import numpy as np
import ml_dtypes


def mxq(x, axis, fmt="e4m3"):
    dtype, down = {"e4m3": (ml_dtypes.float8_e4m3fn, 7), "e5m2": (ml_dtypes.float8_e5m2, 14)}[fmt]
    v = np.moveaxis(np.asarray(x, np.float32).astype(ml_dtypes.bfloat16).astype(np.float64), axis, -1)
    blocks = v.reshape(v.shape[:-1] + (-1, 32))
    amax = np.abs(blocks).max(-1, keepdims=True)
    byte = np.maximum(np.where(amax > 0, np.frexp(amax)[1] - 1 + 127, 0) - down, 1)
    scale = np.exp2(byte - 127.0)
    codes = (blocks / scale).astype(np.float32).astype(dtype).astype(np.float64)
    return np.moveaxis((codes * scale).reshape(v.shape), -1, axis)


WIDE = False


def mx_kscale(k):
    if not WIDE:
        return np.ones(k)
    levels = np.array([10, -10, 5, -5, 0])
    if k % 512:
        return np.exp2(np.random.permutation(np.resize(levels, k // 32))).repeat(32)
    a = np.empty((k // 512, 16))
    for p in range(k // 512):
        a[p, :8] = np.random.permutation(np.resize(levels, 8))
        for g in range(8):
            far = levels[np.abs(levels - a[p, g]) >= 10]
            a[p, g + 8] = far[np.random.randint(len(far))]
    return np.exp2(a.ravel()).repeat(32)


def f64(x):
    return np.asarray(x).astype(np.float64)


def striped(idx):
    return np.tile(idx.reshape(-1, 16).T, (8, 1)).astype(np.uint16)


def unstriped(offs):
    return offs[:16].T.reshape(-1).astype(np.int64)


def pack_weight(w):
    k, n = w.shape
    w = f64(np.asarray(w, np.float32).astype(ml_dtypes.bfloat16)).reshape(k // 32, 32, n)
    amax = np.abs(w).max(1)
    byte = np.clip(np.where(amax > 0, np.frexp(amax)[1] - 1 + 127 - 7, 1), 1, 254)
    scaled = (w * np.exp2(127.0 - byte)[:, None, :]).reshape(k, n).astype(np.float32)
    words = np.ascontiguousarray(scaled.reshape(k // 512, 128, 4, n).transpose(0, 1, 3, 2)).astype(ml_dtypes.float8_e4m3fn).view(np.uint8)
    return words, np.ascontiguousarray(byte.astype(np.uint8).reshape(k // 512, 16, n))


def unpack_weight(words, scales):
    g, p, n, _ = words.shape
    vals = np.ascontiguousarray(words).view(ml_dtypes.float8_e4m3fn).astype(np.float64) * np.repeat(np.exp2(scales.astype(np.float64) - 127.0), 8, axis=1)[..., None]
    return vals.transpose(0, 1, 3, 2).reshape(g * 512, n)


K, T, S, H, N = 512, 1024, 512, 512, 256


def setup_inputs():
    n = np.random.standard_normal
    s = mx_kscale(K)[:, None]
    u = mx_kscale(H)
    packed_xT = pack_weight(n((K, T)) * s)
    packed_gT = pack_weight(n((K, T)) * s)
    packed_dT = pack_weight(n((K, T)) * s)
    packed_eT = pack_weight(n((K, T)) * s)
    return {
        "x_words": packed_xT[0],
        "x_scales": packed_xT[1],
        "g_words": packed_gT[0],
        "g_scales": packed_gT[1],
        "d_words": packed_dT[0],
        "d_scales": packed_dT[1],
        "e_words": packed_eT[0],
        "e_scales": packed_eT[1],
        "w1": (n((K, H)) / np.sqrt(K) / s).astype(np.float32),
        "w2": (n((K, N)) / np.sqrt(K) / s).astype(np.float32),
        "w3": (n((K, N)) / np.sqrt(K) / s).astype(np.float32),
        "w4": (n((H, N)) / np.sqrt(2 * H) / u[:, None]).astype(np.float32),
        "w5": (n((K, N)) / np.sqrt(2 * K) / s).astype(np.float32),
        "gain": (np.random.uniform(0.5, 1.0, (H, 1)) * u[:, None]).astype(np.float32),
        "skip": (n((N, S))).astype(np.float32),
        "offs": striped(np.random.permutation(T)[:S]),
    }


def reference(x_words, x_scales, g_words, g_scales, d_words, d_scales, e_words, e_scales, w1, w2, w3, w4, w5, gain, skip, offs):
    xq = unpack_weight(x_words, x_scales)[:, unstriped(offs)]
    w1q = mxq(f64(w1), 0, "e4m3")
    vx = w1q.T @ xq
    g_offs = unpack_weight(g_words, g_scales)[:, unstriped(offs)]
    vy = w1q.T @ g_offs
    d_offs = unpack_weight(d_words, d_scales)[:, unstriped(offs)]
    vz = w1q.T @ d_offs
    nrm = f64(gain) * (np.sqrt((vx) ** 2 + (vy) ** 2 + (vz) ** 2 + 0.05))
    e_offs = unpack_weight(e_words, e_scales)[:, unstriped(offs)]
    gate = mxq(f64(w4), 0, "e4m3").T @ mxq(nrm, 0, "e4m3") + mxq(f64(w5), 0, "e4m3").T @ e_offs
    w2q = mxq(f64(w2), 0, "e4m3")
    ax = w2q.T @ xq
    w3q = mxq(f64(w3), 0, "e4m3")
    bx = w3q.T @ xq
    ay = w2q.T @ g_offs
    by = w3q.T @ g_offs
    az = w2q.T @ d_offs
    bz = w3q.T @ d_offs
    dot = ax * bx + ay * by + az * bz
    return gate * (0.5 * dot) + f64(skip)

@@ -1,0 +1,254 @@
+from contextlib import ExitStack
+
+import concourse.mybir as mybir
+from concourse.masks import make_identity
+
+K, T, S, H, N = 512, 1024, 512, 512, 256
+FLOPS = 2 * K * S * (3 * H + 6 * N + 2 * N)
+
+F32 = mybir.dt.float32
+BF16 = mybir.dt.bfloat16
+I32 = mybir.dt.int32
+U32 = mybir.dt.uint32
+U16 = mybir.dt.uint16
+U8 = mybir.dt.uint8
+FP8X4 = mybir.dt.float8_e4m3fn_x4
+ACT = mybir.ActivationFunctionType
+ALU = mybir.AluOpType
+
+P = 128
+PACK = 4
+HALF = S // 2
+TILES = S // P
+EPS = 0.05
+
+
+def tile_picked_ypainn_none_p_kernel(
+    tc, x_words, x_scales, g_words, g_scales, d_words, d_scales, e_words, e_scales,
+    w1, w2, w3, w4, w5, gain, skip, offs, out,
+):
+    nc = tc.nc
+    with ExitStack() as ctx:
+        keep = ctx.enter_context(tc.tile_pool(name="keep", bufs=1))
+        ring = ctx.enter_context(tc.tile_pool(name="ring", bufs=3))
+        proj_banks = ctx.enter_context(tc.psum_pool(name="proj_banks", bufs=5))
+        sum_banks = ctx.enter_context(tc.psum_pool(name="sum_banks", bufs=1))
+        end_banks = ctx.enter_context(tc.psum_pool(name="end_banks", bufs=1))
+
+        words_in = {"x": x_words, "g": g_words, "d": d_words, "e": e_words}
+        scales_in = {"x": x_scales, "g": g_scales, "d": d_scales, "e": e_scales}
+        word_win, scale_win, codes, planes = {}, {}, {}, {}
+        raw, grouped = {}, {}
+
+        offsets = keep.tile([P, S // 16], U16, name="offsets")
+        nc.sync.dma_start(offsets[:], offs)
+
+        for c in "xgde":
+            scale_win[c] = keep.tile([P, T], U8, name="scale_win_" + c, align_bytes=64)
+            nc.vector.memset(scale_win[c][:].bitcast(I32), 0)
+
+        warm = keep.tile([P, 8], F32, name="warm")
+        nc.gpsimd.memset(warm[:, 0:1], 1.0)
+        nc.scalar.activation(out=warm[:, 4:5], in_=warm[:, 0:1], func=ACT.Sqrt)
+
+        ident = keep.tile([P, P], F32, name="ident")
+        make_identity(nc, ident[:])
+
+        def load_scales(c):
+            for q in range(4):
+                nc.sync.dma_start(
+                    out=scale_win[c][32 * q : 32 * q + 4, :].bitcast(I32),
+                    in_=scales_in[c][0, 4 * q : 4 * q + 4, :].bitcast(I32),
+                )
+
+        def load_words(c):
+            word_win[c] = keep.tile([P, T], I32, name="word_win_" + c, align_bytes=64)
+            nc.sync.dma_start(out=word_win[c][:], in_=words_in[c][0].rearrange("p n t -> p (n t)").bitcast(I32))
+
+        def load_weight(name, w):
+            raw[name] = keep.tile([P, PACK, N], F32, name="raw_" + name)
+            nc.sync.dma_start(out=raw[name][:], in_=w.rearrange("(p t) c -> p t c", t=PACK))
+
+        def gather_scales(c):
+            planes[c] = keep.tile([P, S], U8, name="plane_" + c, align_bytes=64)
+            nc.vector.tensor_copy(planes[c][:], scale_win[c][:].indirect(offsets[:]))
+
+        def gather_words(c, h):
+            codes[c, h] = keep.tile([P, HALF], U32, name="codes_%s%d" % (c, h), align_bytes=64)
+            cols = slice(h * HALF // 16, (h + 1) * HALF // 16)
+            nc.vector.tensor_copy(codes[c, h][:], word_win[c][:].bitcast(U32).indirect(offsets[:, cols]))
+
+        def interleave(name, on_vector=False):
+            grouped[name] = keep.tile([P, N, PACK], BF16, name="grouped_" + name, align_bytes=64)
+            dst = grouped[name][:].rearrange("p (c i) t -> p c t i", i=4)
+            src = raw[name][:].rearrange("p t (c i) -> p c t i", i=4)
+            if on_vector:
+                nc.vector.tensor_copy(out=dst, in_=src)
+            else:
+                nc.scalar.copy(out=dst, in_=src)
+
+        w1_codes = keep.tile([P, H], U32, name="w1_codes", align_bytes=64)
+        w1_plane = keep.tile([P, H], U8, name="w1_plane", align_bytes=64)
+        w23_codes = keep.tile([P, 2 * N], U32, name="w23_codes", align_bytes=64)
+        w23_plane = keep.tile([P, 2 * N], U8, name="w23_plane", align_bytes=64)
+        w45_codes = keep.tile([P, 2 * N], U32, name="w45_codes", align_bytes=64)
+        w45_plane = keep.tile([P, 2 * N], U8, name="w45_plane", align_bytes=64)
+        nrm_codes = keep.tile([P, S], U32, name="nrm_codes", align_bytes=64)
+        nrm_plane = keep.tile([P, S], U8, name="nrm_plane", align_bytes=64)
+
+        def quantize_weight(name, w_codes, w_plane, slot):
+            cols = slice(slot * N, (slot + 1) * N)
+            nc.vector.quantize_mx(
+                out=w_codes[:, cols].bitcast(FP8X4),
+                scales=w_plane[:, cols],
+                in_=grouped[name][:].rearrange("p c t -> p (c t)"),
+            )
+
+        def project(c, j, w_codes, w_plane):
+            bank = proj_banks.tile([P, H], F32, name="proj")
+            h, r = divmod(j, 2)
+            nc.tensor.matmul_mx(
+                out=bank[:],
+                lhsT=codes[c, h][:, r * P : (r + 1) * P].bitcast(FP8X4),
+                lhsT_scale=planes[c][:, j * P : (j + 1) * P],
+                rhs=w_codes[:].bitcast(FP8X4),
+                rhs_scale=w_plane[:],
+                start=True,
+                stop=True,
+            )
+            return bank
+
+        squares, products = {}, {}
+
+        def square(c, j):
+            bank = project(c, j, w1_codes, w1_plane)
+            squares[c, j] = keep.tile([P, PACK, P], F32, name="square_%s%d" % (c, j))
+            nc.scalar.activation(
+                out=squares[c, j][:], in_=bank[:].rearrange("a (m t) -> a t m", t=PACK), func=ACT.Square
+            )
+
+        def norm(j):
+            total = sum_banks.tile([P, PACK, P], F32, name="total")
+            for t in range(PACK):
+                for n, c in enumerate("dxg"):
+                    nc.tensor.matmul(
+                        out=total[:, t, :], lhsT=squares[c, j][:, t, :], rhs=ident[:],
+                        is_transpose=True, start=(n == 0), stop=(n == 2),
+                    )
+            root = ring.tile([P, P, PACK], F32, name="root")
+            nc.scalar.activation(out=root[:], in_=total[:].rearrange("p t a -> p a t"), func=ACT.Sqrt, bias=EPS)
+            return root
+
+        def scale_norm(root):
+            nrm = ring.tile([P, P, PACK], BF16, name="nrm", align_bytes=64)
+            nc.vector.tensor_tensor(
+                out=nrm[:], in0=root[:], in1=gain_sb[:].unsqueeze(1).to_broadcast([P, P, PACK]), op=ALU.mult
+            )
+            return nrm
+
+        def quantize_norm(j, nrm):
+            cols = slice(j * P, (j + 1) * P)
+            nc.vector.quantize_mx(
+                out=nrm_codes[:, cols].bitcast(FP8X4),
+                scales=nrm_plane[:, cols],
+                in_=nrm[:].rearrange("p a t -> p (a t)"),
+            )
+
+        def product(c, j):
+            bank = project(c, j, w23_codes, w23_plane)
+            second = ring.tile([P, N], F32, name="second")
+            nc.scalar.copy(out=second[:], in_=bank[:, N:])
+            products[c, j] = keep.tile([P, N], F32, name="product_%s%d" % (c, j))
+            nc.vector.tensor_tensor(out=products[c, j][:], in0=bank[:, :N], in1=second[:], op=ALU.mult)
+
+        def gate_of(tiles):
+            width = P * len(tiles)
+            cols = slice(tiles[0] * P, tiles[0] * P + width)
+            h, r = divmod(tiles[0], 2)
+            bank = end_banks.tile([P, 2, width], F32, name="gate")
+            for m in range(2):
+                w4_cols = slice(m * P, (m + 1) * P)
+                w5_cols = slice(N + m * P, N + (m + 1) * P)
+                nc.tensor.matmul_mx(
+                    out=bank[:, m, :], lhsT=w45_codes[:, w5_cols].bitcast(FP8X4), lhsT_scale=w45_plane[:, w5_cols],
+                    rhs=codes["e", h][:, r * P : r * P + width].bitcast(FP8X4), rhs_scale=planes["e"][:, cols],
+                    start=True, stop=False,
+                )
+                nc.tensor.matmul_mx(
+                    out=bank[:, m, :], lhsT=w45_codes[:, w4_cols].bitcast(FP8X4), lhsT_scale=w45_plane[:, w4_cols],
+                    rhs=nrm_codes[:, cols].bitcast(FP8X4), rhs_scale=nrm_plane[:, cols], start=False, stop=True,
+                )
+            gate = ring.tile([P, 2, width], F32, name="gate_sb")
+            nc.scalar.activation(out=gate[:], in_=bank[:], func=ACT.Copy, scale=0.5)
+            return gate
+
+        def finish(tiles, gate):
+            width = P * len(tiles)
+            cols = slice(tiles[0] * P, tiles[0] * P + width)
+            dot = end_banks.tile([P, 2, width], F32, name="dot")
+            for r, j in enumerate(tiles):
+                for m in range(2):
+                    for n, c in enumerate("dxg"):
+                        nc.tensor.matmul(
+                            out=dot[:, m, r * P : (r + 1) * P], lhsT=products[c, j][:, m * P : (m + 1) * P],
+                            rhs=ident[:], is_transpose=True, start=(n == 0), stop=(n == 2),
+                        )
+            gated = ring.tile([P, 2, width], F32, name="gated")
+            nc.vector.tensor_tensor(out=gated[:], in0=dot[:], in1=gate[:], op=ALU.mult)
+            result = ring.tile([P, 2, width], F32, name="result")
+            nc.vector.tensor_tensor(out=result[:], in0=gated[:], in1=skip_sb[:, :, cols], op=ALU.add)
+            nc.sync.dma_start(out=out.rearrange("(m p) s -> p m s", p=P)[:, :, cols], in_=result[:])
+
+        load_scales("x")
+        gain_sb = keep.tile([P, PACK], F32, name="gain_sb")
+        nc.sync.dma_start(out=gain_sb[:], in_=gain.rearrange("(p t) o -> p (t o)", t=PACK))
+        load_weight("w1a", w1[:, :N])
+        load_words("x")
+        load_weight("w1b", w1[:, N:])
+        load_scales("g")
+        load_weight("w2", w2)
+        load_weight("w3", w3)
+        load_words("g")
+        load_scales("d")
+        load_words("d")
+        load_scales("e")
+        load_weight("w4", w4)
+        load_weight("w5", w5)
+        load_words("e")
+        skip_sb = keep.tile([P, 2, S], F32, name="skip_sb")
+        nc.sync.dma_start(out=skip_sb[:], in_=skip.rearrange("(m p) s -> p m s", p=P))
+
+        interleave("w1a")
+        interleave("w1b")
+        quantize_weight("w1a", w1_codes, w1_plane, 0)
+        quantize_weight("w1b", w1_codes, w1_plane, 1)
+        gather_words("x", 0)
+        gather_scales("x")
+        gather_words("x", 1)
+        interleave("w2")
+        interleave("w3", on_vector=True)
+        quantize_weight("w2", w23_codes, w23_plane, 0)
+        quantize_weight("w3", w23_codes, w23_plane, 1)
+        for c in "gd":
+            gather_scales(c)
+            gather_words(c, 0)
+            gather_words(c, 1)
+        for c in "xgd":
+            for j in range(TILES):
+                square(c, j)
+        for j in range(TILES):
+            quantize_norm(j, scale_norm(norm(j)))
+            product("x", j)
+            product("g", j)
+        gather_scales("e")
+        gather_words("e", 0)
+        gather_words("e", 1)
+        interleave("w4", on_vector=True)
+        interleave("w5")
+        quantize_weight("w4", w45_codes, w45_plane, 0)
+        quantize_weight("w5", w45_codes, w45_plane, 1)
+        for tiles in ([0, 1], [2], [3]):
+            gate = gate_of(tiles)
+            for j in tiles:
+                product("d", j)
+            finish(tiles, gate)

@@ -31,9 +31,14 @@ def tile_picked_ypainn_none_p_kernel(
     with ExitStack() as ctx:
         keep = ctx.enter_context(tc.tile_pool(name="keep", bufs=1))
         ring = ctx.enter_context(tc.tile_pool(name="ring", bufs=3))
-        proj_banks = ctx.enter_context(tc.psum_pool(name="proj_banks", bufs=5))
-        sum_banks = ctx.enter_context(tc.psum_pool(name="sum_banks", bufs=1))
-        end_banks = ctx.enter_context(tc.psum_pool(name="end_banks", bufs=1))
+        psum = ctx.enter_context(tc.psum_pool(name="psum", bufs=1))
+        sum_banks = [psum.tile([P, H], F32, name="sum_bank%d" % j) for j in range(TILES)]
+        mx_banks = [psum.tile([P, H], F32, name="mx_bank%d" % b) for b in range(4)]
+        mx_turns = []
+
+        def next_mx_bank():
+            mx_turns.append(len(mx_turns) % len(mx_banks))
+            return mx_banks[mx_turns[-1]]
 
         words_in = {"x": x_words, "g": g_words, "d": d_words, "e": e_words}
         scales_in = {"x": x_scales, "g": g_scales, "d": d_scales, "e": e_scales}
@@ -78,9 +83,10 @@ def tile_picked_ypainn_none_p_kernel(
             cols = slice(h * HALF // 16, (h + 1) * HALF // 16)
             nc.vector.tensor_copy(codes[c, h][:], word_win[c][:].bitcast(U32).indirect(offsets[:, cols]))
 
-        def interleave(name, on_vector=False):
-            grouped[name] = keep.tile([P, N, PACK], BF16, name="grouped_" + name, align_bytes=64)
-            dst = grouped[name][:].rearrange("p (c i) t -> p c t i", i=4)
+        def interleave(pair, slot, name, on_vector=False):
+            if pair not in grouped:
+                grouped[pair] = keep.tile([P, 2 * N, PACK], BF16, name="grouped_" + pair, align_bytes=64)
+            dst = grouped[pair][:, slot * N : (slot + 1) * N, :].rearrange("p (c i) t -> p c t i", i=4)
             src = raw[name][:].rearrange("p t (c i) -> p c t i", i=4)
             if on_vector:
                 nc.vector.tensor_copy(out=dst, in_=src)
@@ -96,16 +102,12 @@ def tile_picked_ypainn_none_p_kernel(
         nrm_codes = keep.tile([P, S], U32, name="nrm_codes", align_bytes=64)
         nrm_plane = keep.tile([P, S], U8, name="nrm_plane", align_bytes=64)
 
-        def quantize_weight(name, w_codes, w_plane, slot):
-            cols = slice(slot * N, (slot + 1) * N)
+        def quantize_pair(pair, w_codes, w_plane):
             nc.vector.quantize_mx(
-                out=w_codes[:, cols].bitcast(FP8X4),
-                scales=w_plane[:, cols],
-                in_=grouped[name][:].rearrange("p c t -> p (c t)"),
+                out=w_codes[:].bitcast(FP8X4), scales=w_plane[:], in_=grouped[pair][:].rearrange("p c t -> p (c t)")
             )
 
-        def project(c, j, w_codes, w_plane):
-            bank = proj_banks.tile([P, H], F32, name="proj")
+        def project(c, j, w_codes, w_plane, bank):
             h, r = divmod(j, 2)
             nc.tensor.matmul_mx(
                 out=bank[:],
@@ -121,22 +123,24 @@ def tile_picked_ypainn_none_p_kernel(
         squares, products = {}, {}
 
         def square(c, j):
-            bank = project(c, j, w1_codes, w1_plane)
+            bank = project(c, j, w1_codes, w1_plane, sum_banks[j] if c == "g" else next_mx_bank())
             squares[c, j] = keep.tile([P, PACK, P], F32, name="square_%s%d" % (c, j))
             nc.scalar.activation(
                 out=squares[c, j][:], in_=bank[:].rearrange("a (m t) -> a t m", t=PACK), func=ACT.Square
             )
 
-        def norm(j):
-            total = sum_banks.tile([P, PACK, P], F32, name="total")
+        def add_squares(c, j):
             for t in range(PACK):
-                for n, c in enumerate("dxg"):
-                    nc.tensor.matmul(
-                        out=total[:, t, :], lhsT=squares[c, j][:, t, :], rhs=ident[:],
-                        is_transpose=True, start=(n == 0), stop=(n == 2),
-                    )
+                nc.tensor.matmul(
+                    out=sum_banks[j][:, t * P : (t + 1) * P], lhsT=squares[c, j][:, t, :], rhs=ident[:],
+                    is_transpose=True, start=(c == "x" and t == 0), stop=(c == "d" and t == PACK - 1),
+                )
+
+        def norm(j):
             root = ring.tile([P, P, PACK], F32, name="root")
-            nc.scalar.activation(out=root[:], in_=total[:].rearrange("p t a -> p a t"), func=ACT.Sqrt, bias=EPS)
+            nc.scalar.activation(
+                out=root[:], in_=sum_banks[j][:].rearrange("p (t a) -> p a t", t=PACK), func=ACT.Sqrt, bias=EPS
+            )
             return root
 
         def scale_norm(root):
@@ -155,7 +159,7 @@ def tile_picked_ypainn_none_p_kernel(
             )
 
         def product(c, j):
-            bank = project(c, j, w23_codes, w23_plane)
+            bank = project(c, j, w23_codes, w23_plane, next_mx_bank())
             second = ring.tile([P, N], F32, name="second")
             nc.scalar.copy(out=second[:], in_=bank[:, N:])
             products[c, j] = keep.tile([P, N], F32, name="product_%s%d" % (c, j))
@@ -165,90 +169,97 @@ def tile_picked_ypainn_none_p_kernel(
             width = P * len(tiles)
             cols = slice(tiles[0] * P, tiles[0] * P + width)
             h, r = divmod(tiles[0], 2)
-            bank = end_banks.tile([P, 2, width], F32, name="gate")
+            bank = next_mx_bank()
             for m in range(2):
                 w4_cols = slice(m * P, (m + 1) * P)
                 w5_cols = slice(N + m * P, N + (m + 1) * P)
                 nc.tensor.matmul_mx(
-                    out=bank[:, m, :], lhsT=w45_codes[:, w5_cols].bitcast(FP8X4), lhsT_scale=w45_plane[:, w5_cols],
-                    rhs=codes["e", h][:, r * P : r * P + width].bitcast(FP8X4), rhs_scale=planes["e"][:, cols],
-                    start=True, stop=False,
+                    out=bank[:, m * width : (m + 1) * width],
+                    lhsT=w45_codes[:, w4_cols].bitcast(FP8X4), lhsT_scale=w45_plane[:, w4_cols],
+                    rhs=nrm_codes[:, cols].bitcast(FP8X4), rhs_scale=nrm_plane[:, cols], start=True, stop=False,
                 )
                 nc.tensor.matmul_mx(
-                    out=bank[:, m, :], lhsT=w45_codes[:, w4_cols].bitcast(FP8X4), lhsT_scale=w45_plane[:, w4_cols],
-                    rhs=nrm_codes[:, cols].bitcast(FP8X4), rhs_scale=nrm_plane[:, cols], start=False, stop=True,
+                    out=bank[:, m * width : (m + 1) * width],
+                    lhsT=w45_codes[:, w5_cols].bitcast(FP8X4), lhsT_scale=w45_plane[:, w5_cols],
+                    rhs=codes["e", h][:, r * P : r * P + width].bitcast(FP8X4), rhs_scale=planes["e"][:, cols],
+                    start=False, stop=True,
                 )
-            gate = ring.tile([P, 2, width], F32, name="gate_sb")
-            nc.scalar.activation(out=gate[:], in_=bank[:], func=ACT.Copy, scale=0.5)
-            return gate
+            return bank
 
-        def finish(tiles, gate):
+        def dot_of(tiles):
             width = P * len(tiles)
-            cols = slice(tiles[0] * P, tiles[0] * P + width)
-            dot = end_banks.tile([P, 2, width], F32, name="dot")
+            dot = sum_banks[tiles[0]]
             for r, j in enumerate(tiles):
                 for m in range(2):
                     for n, c in enumerate("dxg"):
                         nc.tensor.matmul(
-                            out=dot[:, m, r * P : (r + 1) * P], lhsT=products[c, j][:, m * P : (m + 1) * P],
+                            out=dot[:, m * width + r * P : m * width + (r + 1) * P],
+                            lhsT=products[c, j][:, m * P : (m + 1) * P],
                             rhs=ident[:], is_transpose=True, start=(n == 0), stop=(n == 2),
                         )
-            gated = ring.tile([P, 2, width], F32, name="gated")
-            nc.vector.tensor_tensor(out=gated[:], in0=dot[:], in1=gate[:], op=ALU.mult)
+            half_dot = ring.tile([P, 2 * width], F32, name="half_dot")
+            nc.scalar.activation(out=half_dot[:], in_=dot[:, : 2 * width], func=ACT.Copy, scale=0.5)
+            return half_dot
+
+        def finish(tiles, half_dot, gate):
+            width = P * len(tiles)
+            cols = slice(tiles[0] * P, tiles[0] * P + width)
+            gated = ring.tile([P, 2 * width], F32, name="gated")
+            nc.vector.tensor_tensor(out=gated[:], in0=gate[:, : 2 * width], in1=half_dot[:], op=ALU.mult)
             result = ring.tile([P, 2, width], F32, name="result")
-            nc.vector.tensor_tensor(out=result[:], in0=gated[:], in1=skip_sb[:, :, cols], op=ALU.add)
+            nc.vector.tensor_tensor(
+                out=result[:], in0=gated[:].rearrange("p (m s) -> p m s", m=2), in1=skip_sb[:, :, cols], op=ALU.add
+            )
             nc.sync.dma_start(out=out.rearrange("(m p) s -> p m s", p=P)[:, :, cols], in_=result[:])
 
-        load_scales("x")
-        gain_sb = keep.tile([P, PACK], F32, name="gain_sb")
-        nc.sync.dma_start(out=gain_sb[:], in_=gain.rearrange("(p t) o -> p (t o)", t=PACK))
-        load_weight("w1a", w1[:, :N])
         load_words("x")
+        load_scales("x")
+        load_weight("w1a", w1[:, :N])
         load_weight("w1b", w1[:, N:])
         load_scales("g")
+        load_weight("w4", w4)
+        load_scales("d")
+        load_words("g")
+        load_words("d")
         load_weight("w2", w2)
         load_weight("w3", w3)
-        load_words("g")
-        load_scales("d")
-        load_words("d")
-        load_scales("e")
-        load_weight("w4", w4)
-        load_weight("w5", w5)
         load_words("e")
+        load_scales("e")
+        gain_sb = keep.tile([P, PACK], F32, name="gain_sb")
+        nc.sync.dma_start(out=gain_sb[:], in_=gain.rearrange("(p t) o -> p (t o)", t=PACK))
+        load_weight("w5", w5)
         skip_sb = keep.tile([P, 2, S], F32, name="skip_sb")
         nc.sync.dma_start(out=skip_sb[:], in_=skip.rearrange("(m p) s -> p m s", p=P))
 
-        interleave("w1a")
-        interleave("w1b")
-        quantize_weight("w1a", w1_codes, w1_plane, 0)
-        quantize_weight("w1b", w1_codes, w1_plane, 1)
-        gather_words("x", 0)
-        gather_scales("x")
-        gather_words("x", 1)
-        interleave("w2")
-        interleave("w3", on_vector=True)
-        quantize_weight("w2", w23_codes, w23_plane, 0)
-        quantize_weight("w3", w23_codes, w23_plane, 1)
-        for c in "gd":
+        interleave("w1", 0, "w1a")
+        interleave("w1", 1, "w1b", on_vector=True)
+        quantize_pair("w1", w1_codes, w1_plane)
+        for c in "xgd":
             gather_scales(c)
             gather_words(c, 0)
             gather_words(c, 1)
+        interleave("w23", 0, "w2", on_vector=True)
+        interleave("w23", 1, "w3", on_vector=True)
+        quantize_pair("w23", w23_codes, w23_plane)
         for c in "xgd":
             for j in range(TILES):
                 square(c, j)
         for j in range(TILES):
-            quantize_norm(j, scale_norm(norm(j)))
             product("x", j)
+        for j in range(TILES):
+            add_squares("x", j)
+            add_squares("g", j)
+        for j in range(TILES):
+            add_squares("d", j)
+            quantize_norm(j, scale_norm(norm(j)))
             product("g", j)
+            product("d", j)
         gather_scales("e")
         gather_words("e", 0)
         gather_words("e", 1)
-        interleave("w4", on_vector=True)
-        interleave("w5")
-        quantize_weight("w4", w45_codes, w45_plane, 0)
-        quantize_weight("w5", w45_codes, w45_plane, 1)
+        interleave("w45", 0, "w4")
+        interleave("w45", 1, "w5")
+        quantize_pair("w45", w45_codes, w45_plane)
         for tiles in ([0, 1], [2], [3]):
-            gate = gate_of(tiles)
-            for j in tiles:
-                product("d", j)
-            finish(tiles, gate)
+            half_dot = dot_of(tiles)
+            finish(tiles, half_dot, gate_of(tiles))

@@ -30,7 +30,7 @@ def tile_picked_ypainn_none_p_kernel(
     nc = tc.nc
     with ExitStack() as ctx:
         keep = ctx.enter_context(tc.tile_pool(name="keep", bufs=1))
-        ring = ctx.enter_context(tc.tile_pool(name="ring", bufs=3))
+        ring = ctx.enter_context(tc.tile_pool(name="ring", bufs=4))
         psum = ctx.enter_context(tc.psum_pool(name="psum", bufs=1))
         sum_banks = [psum.tile([P, H], F32, name="sum_bank%d" % j) for j in range(TILES)]
         mx_banks = [psum.tile([P, H], F32, name="mx_bank%d" % b) for b in range(4)]
@@ -123,20 +123,19 @@ def tile_picked_ypainn_none_p_kernel(
         squares, products = {}, {}
 
         def square(c, j):
-            bank = project(c, j, w1_codes, w1_plane, sum_banks[j] if c == "g" else next_mx_bank())
+            bank = project(c, j, w1_codes, w1_plane, next_mx_bank())
             squares[c, j] = keep.tile([P, PACK, P], F32, name="square_%s%d" % (c, j))
             nc.scalar.activation(
                 out=squares[c, j][:], in_=bank[:].rearrange("a (m t) -> a t m", t=PACK), func=ACT.Square
             )
 
-        def add_squares(c, j):
-            for t in range(PACK):
-                nc.tensor.matmul(
-                    out=sum_banks[j][:, t * P : (t + 1) * P], lhsT=squares[c, j][:, t, :], rhs=ident[:],
-                    is_transpose=True, start=(c == "x" and t == 0), stop=(c == "d" and t == PACK - 1),
-                )
-
         def norm(j):
+            for t in range(PACK):
+                for n, c in enumerate("dxg"):
+                    nc.tensor.matmul(
+                        out=sum_banks[j][:, t * P : (t + 1) * P], lhsT=squares[c, j][:, t, :], rhs=ident[:],
+                        is_transpose=True, start=(n == 0), stop=(n == 2),
+                    )
             root = ring.tile([P, P, PACK], F32, name="root")
             nc.scalar.activation(
                 out=root[:], in_=sum_banks[j][:].rearrange("p (t a) -> p a t", t=PACK), func=ACT.Sqrt, bias=EPS
@@ -216,17 +215,17 @@ def tile_picked_ypainn_none_p_kernel(
         load_scales("x")
         load_weight("w1a", w1[:, :N])
         load_weight("w1b", w1[:, N:])
-        load_scales("g")
-        load_weight("w4", w4)
-        load_scales("d")
-        load_words("g")
-        load_words("d")
         load_weight("w2", w2)
+        load_scales("g")
+        load_words("g")
+        load_scales("d")
+        load_words("d")
         load_weight("w3", w3)
-        load_words("e")
         load_scales("e")
+        load_words("e")
         gain_sb = keep.tile([P, PACK], F32, name="gain_sb")
         nc.sync.dma_start(out=gain_sb[:], in_=gain.rearrange("(p t) o -> p (t o)", t=PACK))
+        load_weight("w4", w4)
         load_weight("w5", w5)
         skip_sb = keep.tile([P, 2, S], F32, name="skip_sb")
         nc.sync.dma_start(out=skip_sb[:], in_=skip.rearrange("(m p) s -> p m s", p=P))
@@ -238,7 +237,7 @@ def tile_picked_ypainn_none_p_kernel(
             gather_scales(c)
             gather_words(c, 0)
             gather_words(c, 1)
-        interleave("w23", 0, "w2", on_vector=True)
+        interleave("w23", 0, "w2")
         interleave("w23", 1, "w3", on_vector=True)
         quantize_pair("w23", w23_codes, w23_plane)
         for c in "xgd":
@@ -247,10 +246,6 @@ def tile_picked_ypainn_none_p_kernel(
         for j in range(TILES):
             product("x", j)
         for j in range(TILES):
-            add_squares("x", j)
-            add_squares("g", j)
-        for j in range(TILES):
-            add_squares("d", j)
             quantize_norm(j, scale_norm(norm(j)))
             product("g", j)
             product("d", j)

@@ -30,15 +30,13 @@ def tile_picked_ypainn_none_p_kernel(
     nc = tc.nc
     with ExitStack() as ctx:
         keep = ctx.enter_context(tc.tile_pool(name="keep", bufs=1))
-        ring = ctx.enter_context(tc.tile_pool(name="ring", bufs=4))
         psum = ctx.enter_context(tc.psum_pool(name="psum", bufs=1))
-        sum_banks = [psum.tile([P, H], F32, name="sum_bank%d" % j) for j in range(TILES)]
-        mx_banks = [psum.tile([P, H], F32, name="mx_bank%d" % b) for b in range(4)]
-        mx_turns = []
+        banks = [psum.tile([P, H], F32, name="bank%d" % b) for b in range(8)]
 
-        def next_mx_bank():
-            mx_turns.append(len(mx_turns) % len(mx_banks))
-            return mx_banks[mx_turns[-1]]
+        shared = {"scale_win_e": "a", "product_x": "a", "root0": "b", "product_g": "b", "root1": "c", "product_d": "c"}
+
+        def sbuf(shape, dtype, name, align_bytes=64):
+            return keep.tile(shape, dtype, name=name, tag=shared.get(name, name), align_bytes=64)
 
         words_in = {"x": x_words, "g": g_words, "d": d_words, "e": e_words}
         scales_in = {"x": x_scales, "g": g_scales, "d": d_scales, "e": e_scales}
@@ -48,213 +46,289 @@ def tile_picked_ypainn_none_p_kernel(
         offsets = keep.tile([P, S // 16], U16, name="offsets")
         nc.sync.dma_start(offsets[:], offs)
 
-        for c in "xgde":
-            scale_win[c] = keep.tile([P, T], U8, name="scale_win_" + c, align_bytes=64)
-            nc.vector.memset(scale_win[c][:].bitcast(I32), 0)
+        def clear_scales(c, engine):
+            scale_win[c] = sbuf([P, T], U8, name="scale_win_" + c, align_bytes=64)
+            engine.memset(scale_win[c][:].bitcast(I32), 0)
 
-        warm = keep.tile([P, 8], F32, name="warm")
-        nc.gpsimd.memset(warm[:, 0:1], 1.0)
-        nc.scalar.activation(out=warm[:, 4:5], in_=warm[:, 0:1], func=ACT.Sqrt)
+        def load_scales(c, queue):
+            rows = scales_in[c][0].bitcast(I32)
+            for r in range(4):
+                queue.dma_start(out=scale_win[c][r:P:32, :].bitcast(I32), in_=rows[r:16:4, :])
 
-        ident = keep.tile([P, P], F32, name="ident")
-        make_identity(nc, ident[:])
-
-        def load_scales(c):
+        def load_scales_q(c, queue):
             for q in range(4):
-                nc.sync.dma_start(
+                queue.dma_start(
                     out=scale_win[c][32 * q : 32 * q + 4, :].bitcast(I32),
                     in_=scales_in[c][0, 4 * q : 4 * q + 4, :].bitcast(I32),
                 )
 
         def load_words(c):
-            word_win[c] = keep.tile([P, T], I32, name="word_win_" + c, align_bytes=64)
+            word_win[c] = sbuf([P, T], I32, name="word_win_" + c, align_bytes=64)
             nc.sync.dma_start(out=word_win[c][:], in_=words_in[c][0].rearrange("p n t -> p (n t)").bitcast(I32))
 
         def load_weight(name, w):
-            raw[name] = keep.tile([P, PACK, N], F32, name="raw_" + name)
+            raw[name] = sbuf([P, PACK, N], F32, name="raw_" + name)
             nc.sync.dma_start(out=raw[name][:], in_=w.rearrange("(p t) c -> p t c", t=PACK))
 
         def gather_scales(c):
-            planes[c] = keep.tile([P, S], U8, name="plane_" + c, align_bytes=64)
+            planes[c] = sbuf([P, S], U8, name="plane_" + c, align_bytes=64)
             nc.vector.tensor_copy(planes[c][:], scale_win[c][:].indirect(offsets[:]))
 
         def gather_words(c, h):
-            codes[c, h] = keep.tile([P, HALF], U32, name="codes_%s%d" % (c, h), align_bytes=64)
+            codes[c, h] = sbuf([P, HALF], U32, name="codes_%s%d" % (c, h), align_bytes=64)
             cols = slice(h * HALF // 16, (h + 1) * HALF // 16)
             nc.vector.tensor_copy(codes[c, h][:], word_win[c][:].bitcast(U32).indirect(offsets[:, cols]))
 
-        def interleave(pair, slot, name, on_vector=False):
+        def interleave(pair, slot, name, engine):
             if pair not in grouped:
-                grouped[pair] = keep.tile([P, 2 * N, PACK], BF16, name="grouped_" + pair, align_bytes=64)
+                grouped[pair] = sbuf([P, 2 * N, PACK], BF16, name="grouped_" + pair, align_bytes=64)
             dst = grouped[pair][:, slot * N : (slot + 1) * N, :].rearrange("p (c i) t -> p c t i", i=4)
             src = raw[name][:].rearrange("p t (c i) -> p c t i", i=4)
-            if on_vector:
+            if engine == "V":
                 nc.vector.tensor_copy(out=dst, in_=src)
+            elif engine == "G":
+                nc.gpsimd.tensor_scalar(
+                    out=grouped[pair][:, slot * N : (slot + 1) * N, :], in0=raw[name][:].rearrange("p t c -> p c t"),
+                    scalar1=1.0, scalar2=0.0, op0=ALU.mult, op1=ALU.add,
+                )
             else:
                 nc.scalar.copy(out=dst, in_=src)
 
-        w1_codes = keep.tile([P, H], U32, name="w1_codes", align_bytes=64)
-        w1_plane = keep.tile([P, H], U8, name="w1_plane", align_bytes=64)
-        w23_codes = keep.tile([P, 2 * N], U32, name="w23_codes", align_bytes=64)
-        w23_plane = keep.tile([P, 2 * N], U8, name="w23_plane", align_bytes=64)
-        w45_codes = keep.tile([P, 2 * N], U32, name="w45_codes", align_bytes=64)
-        w45_plane = keep.tile([P, 2 * N], U8, name="w45_plane", align_bytes=64)
-        nrm_codes = keep.tile([P, S], U32, name="nrm_codes", align_bytes=64)
-        nrm_plane = keep.tile([P, S], U8, name="nrm_plane", align_bytes=64)
+        w_codes = {n: sbuf([P, 2 * N], U32, name=n + "_codes", align_bytes=64) for n in ("w1", "w23", "w45", "nrm")}
+        w_plane = {n: sbuf([P, 2 * N], U8, name=n + "_plane", align_bytes=64) for n in ("w1", "w23", "w45", "nrm")}
 
-        def quantize_pair(pair, w_codes, w_plane):
+        def quantize_pair(pair):
             nc.vector.quantize_mx(
-                out=w_codes[:].bitcast(FP8X4), scales=w_plane[:], in_=grouped[pair][:].rearrange("p c t -> p (c t)")
+                out=w_codes[pair][:].bitcast(FP8X4), scales=w_plane[pair][:],
+                in_=grouped[pair][:].rearrange("p c t -> p (c t)"),
             )
 
-        def project(c, j, w_codes, w_plane, bank):
+        def project(c, j, pair, cols, dst):
             h, r = divmod(j, 2)
             nc.tensor.matmul_mx(
-                out=bank[:],
+                out=dst,
                 lhsT=codes[c, h][:, r * P : (r + 1) * P].bitcast(FP8X4),
                 lhsT_scale=planes[c][:, j * P : (j + 1) * P],
-                rhs=w_codes[:].bitcast(FP8X4),
-                rhs_scale=w_plane[:],
+                rhs=w_codes[pair][:, cols].bitcast(FP8X4),
+                rhs_scale=w_plane[pair][:, cols],
                 start=True,
                 stop=True,
             )
-            return bank
 
-        squares, products = {}, {}
+        squares, products, seconds, roots, half_gates, gateds = {}, {}, {}, {}, {}, {}
 
-        def square(c, j):
-            bank = project(c, j, w1_codes, w1_plane, next_mx_bank())
-            squares[c, j] = keep.tile([P, PACK, P], F32, name="square_%s%d" % (c, j))
+        def project_w1(c, j, bank):
+            project(c, j, "w1", slice(0, H), bank[:])
+
+        def square(c, j, bank):
+            squares[c, j] = sbuf([P, PACK, P], F32, name="square_%s%d" % (c, j))
             nc.scalar.activation(
                 out=squares[c, j][:], in_=bank[:].rearrange("a (m t) -> a t m", t=PACK), func=ACT.Square
             )
 
-        def norm(j):
-            for t in range(PACK):
-                for n, c in enumerate("dxg"):
+        def add_squares(cs, j, bank):
+            first, last = "g" in cs, "d" in cs
+            for c in cs:
+                for t in range(PACK):
                     nc.tensor.matmul(
-                        out=sum_banks[j][:, t * P : (t + 1) * P], lhsT=squares[c, j][:, t, :], rhs=ident[:],
-                        is_transpose=True, start=(n == 0), stop=(n == 2),
+                        out=bank[:, t * P : (t + 1) * P], lhsT=squares[c, j][:, t, :], rhs=ident[:],
+                        is_transpose=True, start=(first and c == cs[0] and t == 0), stop=(last and c == cs[-1] and t == PACK - 1),
                     )
-            root = ring.tile([P, P, PACK], F32, name="root")
+
+        def root_of(j, bank):
+            roots[j] = sbuf([P, P, PACK], F32, name="root%d" % j)
             nc.scalar.activation(
-                out=root[:], in_=sum_banks[j][:].rearrange("p (t a) -> p a t", t=PACK), func=ACT.Sqrt, bias=EPS
+                out=roots[j][:], in_=bank[:].rearrange("p (t a) -> p a t", t=PACK), func=ACT.Sqrt, bias=EPS
             )
-            return root
 
-        def scale_norm(root):
-            nrm = ring.tile([P, P, PACK], BF16, name="nrm", align_bytes=64)
-            nc.vector.tensor_tensor(
-                out=nrm[:], in0=root[:], in1=gain_sb[:].unsqueeze(1).to_broadcast([P, P, PACK]), op=ALU.mult
+        nrm = sbuf([P, S, PACK], BF16, name="nrm", align_bytes=64)
+
+        def scale_norm(j, engine):
+            engine.tensor_tensor(
+                out=nrm[:, j * P : (j + 1) * P, :], in0=roots[j][:],
+                in1=gain_sb[:].unsqueeze(1).to_broadcast([P, P, PACK]), op=ALU.mult,
             )
-            return nrm
 
-        def quantize_norm(j, nrm):
-            cols = slice(j * P, (j + 1) * P)
+        def quantize_norm(j0, j1):
+            cols = slice(j0 * P, j1 * P)
             nc.vector.quantize_mx(
-                out=nrm_codes[:, cols].bitcast(FP8X4),
-                scales=nrm_plane[:, cols],
-                in_=nrm[:].rearrange("p a t -> p (a t)"),
+                out=w_codes["nrm"][:, cols].bitcast(FP8X4),
+                scales=w_plane["nrm"][:, cols],
+                in_=nrm[:, cols, :].rearrange("p a t -> p (a t)"),
             )
 
-        def product(c, j):
-            bank = project(c, j, w23_codes, w23_plane, next_mx_bank())
-            second = ring.tile([P, N], F32, name="second")
-            nc.scalar.copy(out=second[:], in_=bank[:, N:])
-            products[c, j] = keep.tile([P, N], F32, name="product_%s%d" % (c, j))
-            nc.vector.tensor_tensor(out=products[c, j][:], in0=bank[:, :N], in1=second[:], op=ALU.mult)
+        def project_pair(c, h, bank_a, bank_b):
+            for bank, cols in ((bank_b, slice(N, 2 * N)), (bank_a, slice(0, N))):
+                for r in range(2):
+                    project(c, 2 * h + r, "w23", cols, bank[:, r * N : (r + 1) * N])
 
-        def gate_of(tiles):
-            width = P * len(tiles)
-            cols = slice(tiles[0] * P, tiles[0] * P + width)
-            h, r = divmod(tiles[0], 2)
-            bank = next_mx_bank()
+        def copy_second(c, h, bank_b):
+            seconds[c, h] = sbuf([P, 2 * N], F32, name="second_%s%d" % (c, h))
+            nc.scalar.copy(out=seconds[c, h][:], in_=bank_b[:])
+
+        def multiply(c, h, bank_a):
+            if c not in products:
+                products[c] = sbuf([P, TILES, N], F32, name="product_" + c)
+            nc.vector.tensor_tensor(
+                out=products[c][:, 2 * h : 2 * h + 2, :].rearrange("p j m -> p (j m)"),
+                in0=bank_a[:], in1=seconds[c, h][:], op=ALU.mult,
+            )
+
+        def gate_of(h, bank):
+            cols = slice(h * HALF, (h + 1) * HALF)
             for m in range(2):
                 w4_cols = slice(m * P, (m + 1) * P)
                 w5_cols = slice(N + m * P, N + (m + 1) * P)
                 nc.tensor.matmul_mx(
-                    out=bank[:, m * width : (m + 1) * width],
-                    lhsT=w45_codes[:, w4_cols].bitcast(FP8X4), lhsT_scale=w45_plane[:, w4_cols],
-                    rhs=nrm_codes[:, cols].bitcast(FP8X4), rhs_scale=nrm_plane[:, cols], start=True, stop=False,
+                    out=bank[:, m * HALF : (m + 1) * HALF],
+                    lhsT=w_codes["w45"][:, w5_cols].bitcast(FP8X4), lhsT_scale=w_plane["w45"][:, w5_cols],
+                    rhs=codes["e", h][:].bitcast(FP8X4), rhs_scale=planes["e"][:, cols],
+                    start=True, stop=False,
                 )
                 nc.tensor.matmul_mx(
-                    out=bank[:, m * width : (m + 1) * width],
-                    lhsT=w45_codes[:, w5_cols].bitcast(FP8X4), lhsT_scale=w45_plane[:, w5_cols],
-                    rhs=codes["e", h][:, r * P : r * P + width].bitcast(FP8X4), rhs_scale=planes["e"][:, cols],
+                    out=bank[:, m * HALF : (m + 1) * HALF],
+                    lhsT=w_codes["w45"][:, w4_cols].bitcast(FP8X4), lhsT_scale=w_plane["w45"][:, w4_cols],
+                    rhs=w_codes["nrm"][:, cols].bitcast(FP8X4), rhs_scale=w_plane["nrm"][:, cols],
                     start=False, stop=True,
                 )
-            return bank
 
-        def dot_of(tiles):
+        def halve_gate(h, bank):
+            half_gates[h] = sbuf([P, 2, HALF], F32, name="half_gate%d" % h)
+            nc.scalar.activation(
+                out=half_gates[h][:].rearrange("p m s -> p (m s)"), in_=bank[:], func=ACT.Copy, scale=0.5
+            )
+
+        def add_products(cs, tiles, bank):
             width = P * len(tiles)
-            dot = sum_banks[tiles[0]]
-            for r, j in enumerate(tiles):
-                for m in range(2):
-                    for n, c in enumerate("dxg"):
+            for c in cs:
+                for r, j in enumerate(tiles):
+                    for m in range(2):
                         nc.tensor.matmul(
-                            out=dot[:, m * width + r * P : m * width + (r + 1) * P],
-                            lhsT=products[c, j][:, m * P : (m + 1) * P],
-                            rhs=ident[:], is_transpose=True, start=(n == 0), stop=(n == 2),
+                            out=bank[:, m * width + r * P : m * width + (r + 1) * P],
+                            lhsT=products[c][:, j, m * P : (m + 1) * P], rhs=ident[:], is_transpose=True,
+                            start=(c == cs[0] and r == 0 and m == 0),
+                            stop=(c == cs[-1] and r == len(tiles) - 1 and m == 1),
                         )
-            half_dot = ring.tile([P, 2 * width], F32, name="half_dot")
-            nc.scalar.activation(out=half_dot[:], in_=dot[:, : 2 * width], func=ACT.Copy, scale=0.5)
-            return half_dot
 
-        def finish(tiles, half_dot, gate):
+        def gate_dot(tiles, bank):
+            width = P * len(tiles)
+            h, r = divmod(tiles[0], 2)
+            gated = sbuf([P, 2, width], F32, name="gated%d" % tiles[0])
+            nc.vector.tensor_tensor(
+                out=gated[:], in0=bank[:, : 2 * width].rearrange("p (m s) -> p m s", m=2),
+                in1=half_gates[h][:, :, r * P : r * P + width], op=ALU.mult,
+            )
+            gateds[tiles[0]] = gated
+
+        def add_skip(tiles, engine):
             width = P * len(tiles)
             cols = slice(tiles[0] * P, tiles[0] * P + width)
-            gated = ring.tile([P, 2 * width], F32, name="gated")
-            nc.vector.tensor_tensor(out=gated[:], in0=gate[:, : 2 * width], in1=half_dot[:], op=ALU.mult)
-            result = ring.tile([P, 2, width], F32, name="result")
-            nc.vector.tensor_tensor(
-                out=result[:], in0=gated[:].rearrange("p (m s) -> p m s", m=2), in1=skip_sb[:, :, cols], op=ALU.add
-            )
+            gated = gateds[tiles[0]]
+            result = sbuf([P, 2, width], F32, name="result%d" % tiles[0])
+            engine.tensor_tensor(out=result[:], in0=gated[:], in1=skip_sb[:, :, cols], op=ALU.add)
             nc.sync.dma_start(out=out.rearrange("(m p) s -> p m s", p=P)[:, :, cols], in_=result[:])
 
+        def load_gain():
+            tile = sbuf([P, PACK], F32, name="gain_sb")
+            nc.sync.dma_start(out=tile[:], in_=gain.rearrange("(p t) o -> p (t o)", t=PACK))
+            return tile
+
+        def load_skip():
+            tile = sbuf([P, 2, S], F32, name="skip_sb")
+            nc.sync.dma_start(out=tile[:], in_=skip.rearrange("(m p) s -> p m s", p=P))
+            return tile
+
+        def warm_up():
+            warm = sbuf([P, 8], F32, name="warm")
+            nc.vector.memset(warm[:, 0:1], 1.0)
+            nc.scalar.activation(out=warm[:, 4:5], in_=warm[:, 0:1], func=ACT.Sqrt)
+
+        ident = sbuf([P, P], F32, name="ident")
+
+
+        warm_up()
+        clear_scales("x", nc.vector)
+        clear_scales("g", nc.vector)
+        clear_scales("d", nc.vector)
+        clear_scales("e", nc.vector)
+        make_identity(nc, ident[:])
         load_words("x")
-        load_scales("x")
+        load_scales_q("x", nc.sync)
         load_weight("w1a", w1[:, :N])
         load_weight("w1b", w1[:, N:])
         load_weight("w2", w2)
-        load_scales("g")
+        load_scales_q("g", nc.sync)
         load_words("g")
-        load_scales("d")
-        load_words("d")
+        load_scales_q("d", nc.sync)
         load_weight("w3", w3)
-        load_scales("e")
-        load_words("e")
-        gain_sb = keep.tile([P, PACK], F32, name="gain_sb")
-        nc.sync.dma_start(out=gain_sb[:], in_=gain.rearrange("(p t) o -> p (t o)", t=PACK))
+        load_words("d")
+        load_scales("e", nc.sync)
         load_weight("w4", w4)
         load_weight("w5", w5)
-        skip_sb = keep.tile([P, 2, S], F32, name="skip_sb")
-        nc.sync.dma_start(out=skip_sb[:], in_=skip.rearrange("(m p) s -> p m s", p=P))
+        load_words("e")
+        gain_sb = load_gain()
+        skip_sb = load_skip()
 
-        interleave("w1", 0, "w1a")
-        interleave("w1", 1, "w1b", on_vector=True)
-        quantize_pair("w1", w1_codes, w1_plane)
-        for c in "xgd":
+        interleave("w1", 0, "w1a", "S")
+        interleave("w1", 1, "w1b", "V")
+        quantize_pair("w1")
+        interleave("w23", 0, "w2", "S")
+        interleave("w23", 1, "w3", "V")
+        quantize_pair("w23")
+        for c in "xgde":
             gather_scales(c)
             gather_words(c, 0)
             gather_words(c, 1)
-        interleave("w23", 0, "w2")
-        interleave("w23", 1, "w3", on_vector=True)
-        quantize_pair("w23", w23_codes, w23_plane)
-        for c in "xgd":
+        interleave("w45", 0, "w4", "G")
+        interleave("w45", 1, "w5", "G")
+        quantize_pair("w45")
+        for n, c in enumerate("xg"):
             for j in range(TILES):
-                square(c, j)
-        for j in range(TILES):
-            product("x", j)
-        for j in range(TILES):
-            quantize_norm(j, scale_norm(norm(j)))
-            product("g", j)
-            product("d", j)
-        gather_scales("e")
-        gather_words("e", 0)
-        gather_words("e", 1)
-        interleave("w45", 0, "w4")
-        interleave("w45", 1, "w5")
-        quantize_pair("w45", w45_codes, w45_plane)
-        for tiles in ([0, 1], [2], [3]):
-            half_dot = dot_of(tiles)
-            finish(tiles, half_dot, gate_of(tiles))
+                project_w1(c, j, banks[4 * n + j])
+                square(c, j, banks[4 * n + j])
+        add_squares("gx", 0, banks[0])
+        add_squares("gx", 1, banks[1])
+        for h in range(2):
+            project_pair("x", h, banks[2 + 2 * h], banks[3 + 2 * h])
+            copy_second("x", h, banks[3 + 2 * h])
+            multiply("x", h, banks[2 + 2 * h])
+        for j, b in enumerate((6, 7, 3, 5)):
+            project_w1("d", j, banks[b])
+            square("d", j, banks[b])
+        for j in range(2):
+            add_squares("d", j, banks[j])
+            root_of(j, banks[j])
+            scale_norm(j, nc.vector)
+        project_pair("g", 0, banks[6], banks[7])
+        copy_second("g", 0, banks[7])
+        multiply("g", 0, banks[6])
+        quantize_norm(0, 2)
+        add_squares("gxd", 2, banks[2])
+        root_of(2, banks[2])
+        scale_norm(2, nc.vector)
+        project_pair("d", 0, banks[0], banks[1])
+        copy_second("d", 0, banks[1])
+        multiply("d", 0, banks[0])
+        add_squares("gxd", 3, banks[4])
+        root_of(3, banks[4])
+        scale_norm(3, nc.vector)
+        project_pair("g", 1, banks[3], banks[5])
+        copy_second("g", 1, banks[5])
+        multiply("g", 1, banks[3])
+        quantize_norm(2, 4)
+        project_pair("d", 1, banks[2], banks[7])
+        copy_second("d", 1, banks[7])
+        multiply("d", 1, banks[2])
+        gate_of(0, banks[1])
+        halve_gate(0, banks[1])
+        add_products("dgx", [0, 1], banks[6])
+        gate_of(1, banks[5])
+        halve_gate(1, banks[5])
+        gate_dot([0, 1], banks[6])
+        add_skip([0, 1], nc.vector)
+        add_products("dgx", [2], banks[3])
+        add_products("dgx", [3], banks[4])
+        gate_dot([2], banks[3])
+        gate_dot([3], banks[4])
+        add_skip([2], nc.vector)
+        add_skip([3], nc.vector)

@@ -33,7 +33,7 @@ def tile_picked_ypainn_none_p_kernel(
         psum = ctx.enter_context(tc.psum_pool(name="psum", bufs=1))
         banks = [psum.tile([P, H], F32, name="bank%d" % b) for b in range(8)]
 
-        shared = {"scale_win_e": "a", "product_x": "a", "root0": "b", "product_g": "b", "root1": "c", "product_d": "c"}
+        shared = {"scale_win_e": "a", "product_x0": "a", "root0": "b", "product_g0": "b", "root1": "c", "product_g1": "c", "grouped_w45": "g", "product_d0": "g", "root3": "h", "product_d1": "h", "scale_win_d": "e", "w23_codes": "e", "result2": "a"}
 
         def sbuf(shape, dtype, name, align_bytes=64):
             return keep.tile(shape, dtype, name=name, tag=shared.get(name, name), align_bytes=64)
@@ -75,9 +75,12 @@ def tile_picked_ypainn_none_p_kernel(
             nc.vector.tensor_copy(planes[c][:], scale_win[c][:].indirect(offsets[:]))
 
         def gather_words(c, h):
-            codes[c, h] = sbuf([P, HALF], U32, name="codes_%s%d" % (c, h), align_bytes=64)
-            cols = slice(h * HALF // 16, (h + 1) * HALF // 16)
-            nc.vector.tensor_copy(codes[c, h][:], word_win[c][:].bitcast(U32).indirect(offsets[:, cols]))
+            if c not in codes:
+                codes[c] = sbuf([P, S], U32, name="codes_" + c, align_bytes=64)
+            lo, hi = (0, S) if h is None else (h * HALF, (h + 1) * HALF)
+            nc.vector.tensor_copy(
+                codes[c][:, lo:hi], word_win[c][:].bitcast(U32).indirect(offsets[:, lo // 16 : hi // 16])
+            )
 
         def interleave(pair, slot, name, engine):
             if pair not in grouped:
@@ -104,10 +107,9 @@ def tile_picked_ypainn_none_p_kernel(
             )
 
         def project(c, j, pair, cols, dst):
-            h, r = divmod(j, 2)
             nc.tensor.matmul_mx(
                 out=dst,
-                lhsT=codes[c, h][:, r * P : (r + 1) * P].bitcast(FP8X4),
+                lhsT=codes[c][:, j * P : (j + 1) * P].bitcast(FP8X4),
                 lhsT_scale=planes[c][:, j * P : (j + 1) * P],
                 rhs=w_codes[pair][:, cols].bitcast(FP8X4),
                 rhs_scale=w_plane[pair][:, cols],
@@ -116,6 +118,13 @@ def tile_picked_ypainn_none_p_kernel(
             )
 
         squares, products, seconds, roots, half_gates, gateds = {}, {}, {}, {}, {}, {}
+
+        def warm_tensor(bank, passes):
+            for n in range(passes):
+                nc.tensor.matmul_mx(
+                    out=bank[:], lhsT=codes["x"][:, :P].bitcast(FP8X4), lhsT_scale=planes["x"][:, :P],
+                    rhs=codes["x"][:].bitcast(FP8X4), rhs_scale=planes["x"][:], start=True, stop=True,
+                )
 
         def project_w1(c, j, bank):
             project(c, j, "w1", slice(0, H), bank[:])
@@ -126,14 +135,24 @@ def tile_picked_ypainn_none_p_kernel(
                 out=squares[c, j][:], in_=bank[:].rearrange("a (m t) -> a t m", t=PACK), func=ACT.Square
             )
 
-        def add_squares(cs, j, bank):
-            first, last = "g" in cs, "d" in cs
+        def add_squares(cs, j, bank, first, last):
             for c in cs:
                 for t in range(PACK):
                     nc.tensor.matmul(
                         out=bank[:, t * P : (t + 1) * P], lhsT=squares[c, j][:, t, :], rhs=ident[:],
                         is_transpose=True, start=(first and c == cs[0] and t == 0), stop=(last and c == cs[-1] and t == PACK - 1),
                     )
+
+        def sum_squares(j, engine):
+            squares["s", j] = sbuf([P, PACK, P], F32, name="square_s%d" % j)
+            engine.tensor_tensor(out=squares["s", j][:], in0=squares["x", j][:], in1=squares["g", j][:], op=ALU.add)
+
+        def sum_products(h):
+            products["s"] = sbuf([P, TILES, N], F32, name="product_s")
+            part = slice(2 * h, 2 * h + 2)
+            nc.vector.tensor_tensor(
+                out=products["s"][:, part, :], in0=products["x"][:, part, :], in1=products["g"][:, part, :], op=ALU.add
+            )
 
         def root_of(j, bank):
             roots[j] = sbuf([P, P, PACK], F32, name="root%d" % j)
@@ -167,10 +186,12 @@ def tile_picked_ypainn_none_p_kernel(
             nc.scalar.copy(out=seconds[c, h][:], in_=bank_b[:])
 
         def multiply(c, h, bank_a):
-            if c not in products:
-                products[c] = sbuf([P, TILES, N], F32, name="product_" + c)
+            key = c if c == "x" else (c, h)
+            if key not in products:
+                products[key] = sbuf([P, TILES if c == "x" else 2, N], F32, name="product_%s%d" % (c, h))
+            part = products[key][:, 2 * h : 2 * h + 2, :] if c == "x" else products[key][:]
             nc.vector.tensor_tensor(
-                out=products[c][:, 2 * h : 2 * h + 2, :].rearrange("p j m -> p (j m)"),
+                out=part.rearrange("p j m -> p (j m)"),
                 in0=bank_a[:], in1=seconds[c, h][:], op=ALU.mult,
             )
 
@@ -182,7 +203,7 @@ def tile_picked_ypainn_none_p_kernel(
                 nc.tensor.matmul_mx(
                     out=bank[:, m * HALF : (m + 1) * HALF],
                     lhsT=w_codes["w45"][:, w5_cols].bitcast(FP8X4), lhsT_scale=w_plane["w45"][:, w5_cols],
-                    rhs=codes["e", h][:].bitcast(FP8X4), rhs_scale=planes["e"][:, cols],
+                    rhs=codes["e"][:, cols].bitcast(FP8X4), rhs_scale=planes["e"][:, cols],
                     start=True, stop=False,
                 )
                 nc.tensor.matmul_mx(
@@ -192,22 +213,26 @@ def tile_picked_ypainn_none_p_kernel(
                     start=False, stop=True,
                 )
 
-        def halve_gate(h, bank):
+        def halve_gate(h, bank, pieces=1):
             half_gates[h] = sbuf([P, 2, HALF], F32, name="half_gate%d" % h)
-            nc.scalar.activation(
-                out=half_gates[h][:].rearrange("p m s -> p (m s)"), in_=bank[:], func=ACT.Copy, scale=0.5
-            )
+            width = HALF // pieces
+            for r in range(pieces):
+                nc.scalar.activation(
+                    out=half_gates[h][:, :, r * width : (r + 1) * width],
+                    in_=bank[:].rearrange("p (m s) -> p m s", m=2)[:, :, r * width : (r + 1) * width],
+                    func=ACT.Copy, scale=0.5,
+                )
 
-        def add_products(cs, tiles, bank):
+        def add_products(cs, tiles, bank, first, last):
             width = P * len(tiles)
             for c in cs:
                 for r, j in enumerate(tiles):
                     for m in range(2):
                         nc.tensor.matmul(
                             out=bank[:, m * width + r * P : m * width + (r + 1) * P],
-                            lhsT=products[c][:, j, m * P : (m + 1) * P], rhs=ident[:], is_transpose=True,
-                            start=(c == cs[0] and r == 0 and m == 0),
-                            stop=(c == cs[-1] and r == len(tiles) - 1 and m == 1),
+                            lhsT=(products[c][:, j] if c == "x" else products[c, j // 2][:, j % 2])[:, m * P : (m + 1) * P], rhs=ident[:], is_transpose=True,
+                            start=(first and c == cs[0] and r == 0 and m == 0),
+                            stop=(last and c == cs[-1] and r == len(tiles) - 1 and m == 1),
                         )
 
         def gate_dot(tiles, bank):
@@ -259,13 +284,13 @@ def tile_picked_ypainn_none_p_kernel(
         load_weight("w2", w2)
         load_scales_q("g", nc.sync)
         load_words("g")
-        load_scales_q("d", nc.sync)
         load_weight("w3", w3)
+        load_scales_q("d", nc.sync)
         load_words("d")
         load_scales("e", nc.sync)
+        load_words("e")
         load_weight("w4", w4)
         load_weight("w5", w5)
-        load_words("e")
         gain_sb = load_gain()
         skip_sb = load_skip()
 
@@ -273,62 +298,70 @@ def tile_picked_ypainn_none_p_kernel(
         interleave("w1", 1, "w1b", "V")
         quantize_pair("w1")
         interleave("w23", 0, "w2", "S")
-        interleave("w23", 1, "w3", "V")
+        interleave("w23", 1, "w3", "G")
         quantize_pair("w23")
         for c in "xgde":
             gather_scales(c)
-            gather_words(c, 0)
-            gather_words(c, 1)
-        interleave("w45", 0, "w4", "G")
-        interleave("w45", 1, "w5", "G")
-        quantize_pair("w45")
+            for h in ((0, 1) if c == "d" else (None,)):
+                gather_words(c, h)
         for n, c in enumerate("xg"):
             for j in range(TILES):
                 project_w1(c, j, banks[4 * n + j])
                 square(c, j, banks[4 * n + j])
-        add_squares("gx", 0, banks[0])
-        add_squares("gx", 1, banks[1])
-        for h in range(2):
-            project_pair("x", h, banks[2 + 2 * h], banks[3 + 2 * h])
-            copy_second("x", h, banks[3 + 2 * h])
-            multiply("x", h, banks[2 + 2 * h])
-        for j, b in enumerate((6, 7, 3, 5)):
+        add_squares("gx", 0, banks[0], True, False)
+        for j in (1, 2):
+            sum_squares(j, nc.gpsimd)
+        for h, (a, b) in enumerate(((2, 3), (4, 5))):
+            project_pair("x", h, banks[a], banks[b])
+            copy_second("x", h, banks[b])
+            multiply("x", h, banks[a])
+
+        interleave("w45", 0, "w4", "G")
+        interleave("w45", 1, "w5", "V")
+        for j, b in enumerate((1, 6, 7, 3)):
             project_w1("d", j, banks[b])
             square("d", j, banks[b])
-        for j in range(2):
-            add_squares("d", j, banks[j])
-            root_of(j, banks[j])
-            scale_norm(j, nc.vector)
-        project_pair("g", 0, banks[6], banks[7])
-        copy_second("g", 0, banks[7])
-        multiply("g", 0, banks[6])
+        add_squares("s", 1, banks[5], True, False)
+        add_squares("d", 0, banks[0], False, True)
+        root_of(0, banks[0])
+        scale_norm(0, nc.vector)
+        quantize_pair("w45")
+        project_pair("g", 0, banks[1], banks[6])
+        copy_second("g", 0, banks[6])
+        add_squares("d", 1, banks[5], False, True)
+        root_of(1, banks[5])
+        scale_norm(1, nc.vector)
+        multiply("g", 0, banks[1])
         quantize_norm(0, 2)
-        add_squares("gxd", 2, banks[2])
+        project_pair("g", 1, banks[3], banks[7])
+        copy_second("g", 1, banks[7])
+        multiply("g", 1, banks[3])
+        add_squares("sd", 2, banks[2], True, True)
         root_of(2, banks[2])
         scale_norm(2, nc.vector)
-        project_pair("d", 0, banks[0], banks[1])
-        copy_second("d", 0, banks[1])
-        multiply("d", 0, banks[0])
-        add_squares("gxd", 3, banks[4])
+        project_pair("d", 0, banks[5], banks[0])
+        copy_second("d", 0, banks[0])
+        multiply("d", 0, banks[5])
+
+        add_squares("gxd", 3, banks[4], True, True)
         root_of(3, banks[4])
         scale_norm(3, nc.vector)
-        project_pair("g", 1, banks[3], banks[5])
-        copy_second("g", 1, banks[5])
-        multiply("g", 1, banks[3])
         quantize_norm(2, 4)
-        project_pair("d", 1, banks[2], banks[7])
-        copy_second("d", 1, banks[7])
+        project_pair("d", 1, banks[2], banks[6])
+        copy_second("d", 1, banks[6])
         multiply("d", 1, banks[2])
-        gate_of(0, banks[1])
-        halve_gate(0, banks[1])
-        add_products("dgx", [0, 1], banks[6])
-        gate_of(1, banks[5])
-        halve_gate(1, banks[5])
-        gate_dot([0, 1], banks[6])
+        add_products("gx", [0, 1], banks[1], True, False)
+        gate_of(0, banks[7])
+        halve_gate(0, banks[7])
+        add_products("d", [0, 1], banks[1], False, True)
+        add_products("gx", [2], banks[3], True, False)
+        gate_of(1, banks[0])
+        halve_gate(1, banks[0], 2)
+        gate_dot([0, 1], banks[1])
         add_skip([0, 1], nc.vector)
-        add_products("dgx", [2], banks[3])
-        add_products("dgx", [3], banks[4])
+        add_products("d", [2], banks[3], False, True)
+        add_products("dgx", [3], banks[5], True, True)
         gate_dot([2], banks[3])
-        gate_dot([3], banks[4])
+        gate_dot([3], banks[5])
         add_skip([2], nc.vector)
         add_skip([3], nc.vector)

@@ -33,7 +33,7 @@ def tile_picked_ypainn_none_p_kernel(
         psum = ctx.enter_context(tc.psum_pool(name="psum", bufs=1))
         banks = [psum.tile([P, H], F32, name="bank%d" % b) for b in range(8)]
 
-        shared = {"scale_win_e": "a", "product_x0": "a", "root0": "b", "product_g0": "b", "root1": "c", "product_g1": "c", "grouped_w45": "g", "product_d0": "g", "root3": "h", "product_d1": "h", "scale_win_d": "e", "w23_codes": "e", "result2": "a"}
+        shared = {"scale_win_e": "a", "product_x0": "a", "result2": "a", "root0": "b", "product_g0": "b", "grouped_w45": "g", "product_g1": "g", "root1": "c", "product_d0": "c", "root3": "h", "product_d1": "h", "scale_win_d": "e", "w23_codes": "e"}
 
         def sbuf(shape, dtype, name, align_bytes=64):
             return keep.tile(shape, dtype, name=name, tag=shared.get(name, name), align_bytes=64)
@@ -100,10 +100,10 @@ def tile_picked_ypainn_none_p_kernel(
         w_codes = {n: sbuf([P, 2 * N], U32, name=n + "_codes", align_bytes=64) for n in ("w1", "w23", "w45", "nrm")}
         w_plane = {n: sbuf([P, 2 * N], U8, name=n + "_plane", align_bytes=64) for n in ("w1", "w23", "w45", "nrm")}
 
-        def quantize_pair(pair):
+        def quantize_pair(pair, lo=0, hi=2 * N):
             nc.vector.quantize_mx(
-                out=w_codes[pair][:].bitcast(FP8X4), scales=w_plane[pair][:],
-                in_=grouped[pair][:].rearrange("p c t -> p (c t)"),
+                out=w_codes[pair][:, lo:hi].bitcast(FP8X4), scales=w_plane[pair][:, lo:hi],
+                in_=grouped[pair][:, lo:hi, :].rearrange("p c t -> p (c t)"),
             )
 
         def project(c, j, pair, cols, dst):
@@ -296,7 +296,8 @@ def tile_picked_ypainn_none_p_kernel(
 
         interleave("w1", 0, "w1a", "S")
         interleave("w1", 1, "w1b", "V")
-        quantize_pair("w1")
+        quantize_pair("w1", 0, N)
+        quantize_pair("w1", N, 2 * N)
         interleave("w23", 0, "w2", "S")
         interleave("w23", 1, "w3", "G")
         quantize_pair("w23")
@@ -330,15 +331,15 @@ def tile_picked_ypainn_none_p_kernel(
         copy_second("g", 0, banks[6])
         add_squares("d", 1, banks[5], False, True)
         root_of(1, banks[5])
-        scale_norm(1, nc.vector)
+        scale_norm(1, nc.gpsimd)
         multiply("g", 0, banks[1])
-        quantize_norm(0, 2)
         project_pair("g", 1, banks[3], banks[7])
         copy_second("g", 1, banks[7])
         multiply("g", 1, banks[3])
         add_squares("sd", 2, banks[2], True, True)
         root_of(2, banks[2])
         scale_norm(2, nc.vector)
+        quantize_norm(0, 2)
         project_pair("d", 0, banks[5], banks[0])
         copy_second("d", 0, banks[0])
         multiply("d", 0, banks[5])
@@ -350,16 +351,14 @@ def tile_picked_ypainn_none_p_kernel(
         project_pair("d", 1, banks[2], banks[6])
         copy_second("d", 1, banks[6])
         multiply("d", 1, banks[2])
-        add_products("gx", [0, 1], banks[1], True, False)
         gate_of(0, banks[7])
         halve_gate(0, banks[7])
-        add_products("d", [0, 1], banks[1], False, True)
-        add_products("gx", [2], banks[3], True, False)
+        add_products("dgx", [0, 1], banks[1], True, True)
         gate_of(1, banks[0])
         halve_gate(1, banks[0], 2)
         gate_dot([0, 1], banks[1])
         add_skip([0, 1], nc.vector)
-        add_products("d", [2], banks[3], False, True)
+        add_products("dgx", [2], banks[3], True, True)
         add_products("dgx", [3], banks[5], True, True)
         gate_dot([2], banks[3])
         gate_dot([3], banks[5])

@@ -33,7 +33,7 @@ def tile_picked_ypainn_none_p_kernel(
         psum = ctx.enter_context(tc.psum_pool(name="psum", bufs=1))
         banks = [psum.tile([P, H], F32, name="bank%d" % b) for b in range(8)]
 
-        shared = {"scale_win_e": "a", "product_x0": "a", "result2": "a", "root0": "b", "product_g0": "b", "grouped_w45": "g", "product_g1": "g", "root1": "c", "product_d0": "c", "root3": "h", "product_d1": "h", "scale_win_d": "e", "w23_codes": "e"}
+        shared = {"scale_win_e": "a", "product_x0": "a", "root0": "b", "product_g0": "b", "grouped_w45": "g", "product_g1": "g", "root1": "c", "product_d0": "c", "root3": "h", "product_d1": "h", "scale_win_d": "e", "w23_codes": "e", "sum_dot": "b"}
 
         def sbuf(shape, dtype, name, align_bytes=64):
             return keep.tile(shape, dtype, name=name, tag=shared.get(name, name), align_bytes=64)
@@ -181,6 +181,30 @@ def tile_picked_ypainn_none_p_kernel(
                 for r in range(2):
                     project(c, 2 * h + r, "w23", cols, bank[:, r * N : (r + 1) * N])
 
+        def project_last(c, bank_a, bank_b):
+            atoms = slice(3 * P, 4 * P)
+            for bank, first in ((bank_b, N), (bank_a, 0)):
+                project(c, 2, "w23", slice(first, first + N), bank[:, :N])
+                for m in range(2):
+                    cols = slice(first + m * P, first + (m + 1) * P)
+                    nc.tensor.matmul_mx(
+                        out=bank[:, N + m * P : N + (m + 1) * P],
+                        lhsT=w_codes["w23"][:, cols].bitcast(FP8X4), lhsT_scale=w_plane["w23"][:, cols],
+                        rhs=codes[c][:, atoms].bitcast(FP8X4), rhs_scale=planes[c][:, atoms],
+                        start=True, stop=True,
+                    )
+
+        def add_last(name, first, second):
+            products[name] = sbuf([P, N], F32, name="sum_" + name)
+            nc.vector.tensor_tensor(out=products[name][:], in0=first, in1=second, op=ALU.add)
+
+        def gate_last(bank):
+            gateds[3] = sbuf([P, 2, P], F32, name="gated3")
+            nc.vector.scalar_tensor_tensor(
+                out=gateds[3][:], in0=bank[:].rearrange("p (m s) -> p m s", m=2)[:, :, P:], scalar=0.5,
+                in1=products["dot"][:].rearrange("p (m s) -> p m s", m=2), op0=ALU.mult, op1=ALU.mult,
+            )
+
         def copy_second(c, h, bank_b):
             seconds[c, h] = sbuf([P, 2 * N], F32, name="second_%s%d" % (c, h))
             nc.scalar.copy(out=seconds[c, h][:], in_=bank_b[:])
@@ -213,10 +237,10 @@ def tile_picked_ypainn_none_p_kernel(
                     start=False, stop=True,
                 )
 
-        def halve_gate(h, bank, pieces=1):
+        def halve_gate(h, bank, pieces=1, count=1):
             half_gates[h] = sbuf([P, 2, HALF], F32, name="half_gate%d" % h)
             width = HALF // pieces
-            for r in range(pieces):
+            for r in range(count):
                 nc.scalar.activation(
                     out=half_gates[h][:, :, r * width : (r + 1) * width],
                     in_=bank[:].rearrange("p (m s) -> p m s", m=2)[:, :, r * width : (r + 1) * width],
@@ -313,7 +337,10 @@ def tile_picked_ypainn_none_p_kernel(
         for j in (1, 2):
             sum_squares(j, nc.gpsimd)
         for h, (a, b) in enumerate(((2, 3), (4, 5))):
-            project_pair("x", h, banks[a], banks[b])
+            if h == 0:
+                project_pair("x", h, banks[a], banks[b])
+            else:
+                project_last("x", banks[a], banks[b])
             copy_second("x", h, banks[b])
             multiply("x", h, banks[a])
 
@@ -333,7 +360,7 @@ def tile_picked_ypainn_none_p_kernel(
         root_of(1, banks[5])
         scale_norm(1, nc.gpsimd)
         multiply("g", 0, banks[1])
-        project_pair("g", 1, banks[3], banks[7])
+        project_last("g", banks[3], banks[7])
         copy_second("g", 1, banks[7])
         multiply("g", 1, banks[3])
         add_squares("sd", 2, banks[2], True, True)
@@ -347,20 +374,21 @@ def tile_picked_ypainn_none_p_kernel(
         add_squares("gxd", 3, banks[4], True, True)
         root_of(3, banks[4])
         scale_norm(3, nc.vector)
+        add_last("xg", products["x"][:, 3], products["g", 1][:, 1])
         quantize_norm(2, 4)
-        project_pair("d", 1, banks[2], banks[6])
+        project_last("d", banks[2], banks[6])
         copy_second("d", 1, banks[6])
         multiply("d", 1, banks[2])
         gate_of(0, banks[7])
         halve_gate(0, banks[7])
-        add_products("dgx", [0, 1], banks[1], True, True)
+        add_products("dxg", [0, 1], banks[1], True, True)
         gate_of(1, banks[0])
-        halve_gate(1, banks[0], 2)
+        halve_gate(1, banks[0], 2, 1)
         gate_dot([0, 1], banks[1])
+        add_last("dot", products["xg"][:], products["d", 1][:, 1])
         add_skip([0, 1], nc.vector)
         add_products("dgx", [2], banks[3], True, True)
-        add_products("dgx", [3], banks[5], True, True)
+        gate_last(banks[0])
         gate_dot([2], banks[3])
-        gate_dot([3], banks[5])
-        add_skip([2], nc.vector)
         add_skip([3], nc.vector)
+        add_skip([2], nc.vector)

@@ -21,6 +21,7 @@ PACK = 4
 HALF = S // 2
 TILES = S // P
 EPS = 0.05
+ROW0 = {"x": 0, "g": 4, "d": 8, "e": 12}
 
 
 def tile_picked_ypainn_none_p_kernel(
@@ -53,12 +54,12 @@ def tile_picked_ypainn_none_p_kernel(
         def load_scales(c, queue):
             rows = scales_in[c][0].bitcast(I32)
             for r in range(4):
-                queue.dma_start(out=scale_win[c][r:P:32, :].bitcast(I32), in_=rows[r:16:4, :])
+                queue.dma_start(out=scale_win[c][ROW0[c] + r : P : 32, :].bitcast(I32), in_=rows[r:16:4, :])
 
         def load_scales_q(c, queue):
             for q in range(4):
                 queue.dma_start(
-                    out=scale_win[c][32 * q : 32 * q + 4, :].bitcast(I32),
+                    out=scale_win[c][32 * q + ROW0[c] : 32 * q + ROW0[c] + 4, :].bitcast(I32),
                     in_=scales_in[c][0, 4 * q : 4 * q + 4, :].bitcast(I32),
                 )
 
@@ -110,7 +111,7 @@ def tile_picked_ypainn_none_p_kernel(
             nc.tensor.matmul_mx(
                 out=dst,
                 lhsT=codes[c][:, j * P : (j + 1) * P].bitcast(FP8X4),
-                lhsT_scale=planes[c][:, j * P : (j + 1) * P],
+                lhsT_scale=planes[c][ROW0[c] :, j * P : (j + 1) * P],
                 rhs=w_codes[pair][:, cols].bitcast(FP8X4),
                 rhs_scale=w_plane[pair][:, cols],
                 start=True,
@@ -190,7 +191,7 @@ def tile_picked_ypainn_none_p_kernel(
                     nc.tensor.matmul_mx(
                         out=bank[:, N + m * P : N + (m + 1) * P],
                         lhsT=w_codes["w23"][:, cols].bitcast(FP8X4), lhsT_scale=w_plane["w23"][:, cols],
-                        rhs=codes[c][:, atoms].bitcast(FP8X4), rhs_scale=planes[c][:, atoms],
+                        rhs=codes[c][:, atoms].bitcast(FP8X4), rhs_scale=planes[c][ROW0[c] :, atoms],
                         start=True, stop=True,
                     )
 
@@ -227,7 +228,7 @@ def tile_picked_ypainn_none_p_kernel(
                 nc.tensor.matmul_mx(
                     out=bank[:, m * HALF : (m + 1) * HALF],
                     lhsT=w_codes["w45"][:, w5_cols].bitcast(FP8X4), lhsT_scale=w_plane["w45"][:, w5_cols],
-                    rhs=codes["e"][:, cols].bitcast(FP8X4), rhs_scale=planes["e"][:, cols],
+                    rhs=codes["e"][:, cols].bitcast(FP8X4), rhs_scale=planes["e"][ROW0["e"] :, cols],
                     start=True, stop=False,
                 )
                 nc.tensor.matmul_mx(

@@ -177,23 +177,29 @@ def tile_picked_ypainn_none_p_kernel(
                 in_=nrm[:, cols, :].rearrange("p a t -> p (a t)"),
             )
 
+        def project_side(c, h, first, bank):
+            for r in range(2):
+                project(c, 2 * h + r, "w23", slice(first, first + N), bank[:, r * N : (r + 1) * N])
+
         def project_pair(c, h, bank_a, bank_b):
-            for bank, cols in ((bank_b, slice(N, 2 * N)), (bank_a, slice(0, N))):
-                for r in range(2):
-                    project(c, 2 * h + r, "w23", cols, bank[:, r * N : (r + 1) * N])
+            project_side(c, h, N, bank_b)
+            project_side(c, h, 0, bank_a)
+
+        def project_last_side(c, first, bank):
+            atoms = slice(3 * P, 4 * P)
+            project(c, 2, "w23", slice(first, first + N), bank[:, :N])
+            for m in range(2):
+                cols = slice(first + m * P, first + (m + 1) * P)
+                nc.tensor.matmul_mx(
+                    out=bank[:, N + m * P : N + (m + 1) * P],
+                    lhsT=w_codes["w23"][:, cols].bitcast(FP8X4), lhsT_scale=w_plane["w23"][:, cols],
+                    rhs=codes[c][:, atoms].bitcast(FP8X4), rhs_scale=planes[c][ROW0[c] :, atoms],
+                    start=True, stop=True,
+                )
 
         def project_last(c, bank_a, bank_b):
-            atoms = slice(3 * P, 4 * P)
-            for bank, first in ((bank_b, N), (bank_a, 0)):
-                project(c, 2, "w23", slice(first, first + N), bank[:, :N])
-                for m in range(2):
-                    cols = slice(first + m * P, first + (m + 1) * P)
-                    nc.tensor.matmul_mx(
-                        out=bank[:, N + m * P : N + (m + 1) * P],
-                        lhsT=w_codes["w23"][:, cols].bitcast(FP8X4), lhsT_scale=w_plane["w23"][:, cols],
-                        rhs=codes[c][:, atoms].bitcast(FP8X4), rhs_scale=planes[c][ROW0[c] :, atoms],
-                        start=True, stop=True,
-                    )
+            project_last_side(c, N, bank_b)
+            project_last_side(c, 0, bank_a)
 
         def add_last(name, first, second):
             products[name] = sbuf([P, N], F32, name="sum_" + name)
@@ -361,18 +367,19 @@ def tile_picked_ypainn_none_p_kernel(
         root_of(1, banks[5])
         scale_norm(1, nc.gpsimd)
         multiply("g", 0, banks[1])
-        project_last("g", banks[3], banks[7])
+        project_last_side("g", N, banks[7])
         copy_second("g", 1, banks[7])
-        multiply("g", 1, banks[3])
         add_squares("sd", 2, banks[2], True, True)
+        project_last_side("g", 0, banks[3])
+        multiply("g", 1, banks[3])
         root_of(2, banks[2])
         scale_norm(2, nc.vector)
         quantize_norm(0, 2)
-        project_pair("d", 0, banks[5], banks[0])
+        project_side("d", 0, N, banks[0])
         copy_second("d", 0, banks[0])
-        multiply("d", 0, banks[5])
-
         add_squares("gxd", 3, banks[4], True, True)
+        project_side("d", 0, 0, banks[5])
+        multiply("d", 0, banks[5])
         root_of(3, banks[4])
         scale_norm(3, nc.vector)
         add_last("xg", products["x"][:, 3], products["g", 1][:, 1])

from contextlib import ExitStack

import concourse.mybir as mybir
from concourse.masks import make_identity

K, T, S, H, N = 512, 1024, 512, 512, 256
FLOPS = 2 * K * S * (3 * H + 6 * N + 2 * N)

F32 = mybir.dt.float32
BF16 = mybir.dt.bfloat16
I32 = mybir.dt.int32
U32 = mybir.dt.uint32
U16 = mybir.dt.uint16
U8 = mybir.dt.uint8
FP8X4 = mybir.dt.float8_e4m3fn_x4
ACT = mybir.ActivationFunctionType
ALU = mybir.AluOpType

P = 128
PACK = 4
HALF = S // 2
TILES = S // P
EPS = 0.05
ROW0 = {"x": 0, "g": 4, "d": 8, "e": 12}


def tile_picked_ypainn_none_p_kernel(
    tc, x_words, x_scales, g_words, g_scales, d_words, d_scales, e_words, e_scales,
    w1, w2, w3, w4, w5, gain, skip, offs, out,
):
    nc = tc.nc
    with ExitStack() as ctx:
        keep = ctx.enter_context(tc.tile_pool(name="keep", bufs=1))
        psum = ctx.enter_context(tc.psum_pool(name="psum", bufs=1))
        banks = [psum.tile([P, H], F32, name="bank%d" % b) for b in range(8)]

        shared = {"scale_win_e": "a", "product_x0": "a", "root0": "b", "product_g0": "b", "grouped_w45": "g", "product_g1": "g", "root1": "c", "product_d0": "c", "root3": "h", "product_d1": "h", "scale_win_d": "e", "w23_codes": "e", "sum_dot": "b"}

        def sbuf(shape, dtype, name, align_bytes=64):
            return keep.tile(shape, dtype, name=name, tag=shared.get(name, name), align_bytes=64)

        words_in = {"x": x_words, "g": g_words, "d": d_words, "e": e_words}
        scales_in = {"x": x_scales, "g": g_scales, "d": d_scales, "e": e_scales}
        word_win, scale_win, codes, planes = {}, {}, {}, {}
        raw, grouped = {}, {}

        offsets = keep.tile([P, S // 16], U16, name="offsets")
        nc.sync.dma_start(offsets[:], offs)

        def clear_scales(c, engine):
            scale_win[c] = sbuf([P, T], U8, name="scale_win_" + c, align_bytes=64)
            engine.memset(scale_win[c][:].bitcast(I32), 0)

        def load_scales(c, queue):
            rows = scales_in[c][0].bitcast(I32)
            for r in range(4):
                queue.dma_start(out=scale_win[c][ROW0[c] + r : P : 32, :].bitcast(I32), in_=rows[r:16:4, :])

        def load_scales_q(c, queue):
            for q in range(4):
                queue.dma_start(
                    out=scale_win[c][32 * q + ROW0[c] : 32 * q + ROW0[c] + 4, :].bitcast(I32),
                    in_=scales_in[c][0, 4 * q : 4 * q + 4, :].bitcast(I32),
                )

        def load_words(c):
            word_win[c] = sbuf([P, T], I32, name="word_win_" + c, align_bytes=64)
            nc.sync.dma_start(out=word_win[c][:], in_=words_in[c][0].rearrange("p n t -> p (n t)").bitcast(I32))

        def load_weight(name, w):
            raw[name] = sbuf([P, PACK, N], F32, name="raw_" + name)
            nc.sync.dma_start(out=raw[name][:], in_=w.rearrange("(p t) c -> p t c", t=PACK))

        def gather_scales(c):
            planes[c] = sbuf([P, S], U8, name="plane_" + c, align_bytes=64)
            nc.vector.tensor_copy(planes[c][:], scale_win[c][:].indirect(offsets[:]))

        def gather_words(c, h):
            if c not in codes:
                codes[c] = sbuf([P, S], U32, name="codes_" + c, align_bytes=64)
            lo, hi = (0, S) if h is None else (h * HALF, (h + 1) * HALF)
            nc.vector.tensor_copy(
                codes[c][:, lo:hi], word_win[c][:].bitcast(U32).indirect(offsets[:, lo // 16 : hi // 16])
            )

        def interleave(pair, slot, name, engine):
            if pair not in grouped:
                grouped[pair] = sbuf([P, 2 * N, PACK], BF16, name="grouped_" + pair, align_bytes=64)
            dst = grouped[pair][:, slot * N : (slot + 1) * N, :].rearrange("p (c i) t -> p c t i", i=4)
            src = raw[name][:].rearrange("p t (c i) -> p c t i", i=4)
            if engine == "V":
                nc.vector.tensor_copy(out=dst, in_=src)
            elif engine == "G":
                nc.gpsimd.tensor_scalar(
                    out=grouped[pair][:, slot * N : (slot + 1) * N, :], in0=raw[name][:].rearrange("p t c -> p c t"),
                    scalar1=1.0, scalar2=0.0, op0=ALU.mult, op1=ALU.add,
                )
            else:
                nc.scalar.copy(out=dst, in_=src)

        w_codes = {n: sbuf([P, 2 * N], U32, name=n + "_codes", align_bytes=64) for n in ("w1", "w23", "w45", "nrm")}
        w_plane = {n: sbuf([P, 2 * N], U8, name=n + "_plane", align_bytes=64) for n in ("w1", "w23", "w45", "nrm")}

        def quantize_pair(pair, lo=0, hi=2 * N):
            nc.vector.quantize_mx(
                out=w_codes[pair][:, lo:hi].bitcast(FP8X4), scales=w_plane[pair][:, lo:hi],
                in_=grouped[pair][:, lo:hi, :].rearrange("p c t -> p (c t)"),
            )

        def project(c, j, pair, cols, dst):
            nc.tensor.matmul_mx(
                out=dst,
                lhsT=codes[c][:, j * P : (j + 1) * P].bitcast(FP8X4),
                lhsT_scale=planes[c][ROW0[c] :, j * P : (j + 1) * P],
                rhs=w_codes[pair][:, cols].bitcast(FP8X4),
                rhs_scale=w_plane[pair][:, cols],
                start=True,
                stop=True,
            )

        squares, products, seconds, roots, half_gates, gateds = {}, {}, {}, {}, {}, {}

        def warm_tensor(bank, passes):
            for n in range(passes):
                nc.tensor.matmul_mx(
                    out=bank[:], lhsT=codes["x"][:, :P].bitcast(FP8X4), lhsT_scale=planes["x"][:, :P],
                    rhs=codes["x"][:].bitcast(FP8X4), rhs_scale=planes["x"][:], start=True, stop=True,
                )

        def project_w1(c, j, bank):
            project(c, j, "w1", slice(0, H), bank[:])

        def square(c, j, bank):
            squares[c, j] = sbuf([P, PACK, P], F32, name="square_%s%d" % (c, j))
            nc.scalar.activation(
                out=squares[c, j][:], in_=bank[:].rearrange("a (m t) -> a t m", t=PACK), func=ACT.Square
            )

        def add_squares(cs, j, bank, first, last):
            for c in cs:
                for t in range(PACK):
                    nc.tensor.matmul(
                        out=bank[:, t * P : (t + 1) * P], lhsT=squares[c, j][:, t, :], rhs=ident[:],
                        is_transpose=True, start=(first and c == cs[0] and t == 0), stop=(last and c == cs[-1] and t == PACK - 1),
                    )

        def sum_squares(j, engine):
            squares["s", j] = sbuf([P, PACK, P], F32, name="square_s%d" % j)
            engine.tensor_tensor(out=squares["s", j][:], in0=squares["x", j][:], in1=squares["g", j][:], op=ALU.add)

        def sum_products(h):
            products["s"] = sbuf([P, TILES, N], F32, name="product_s")
            part = slice(2 * h, 2 * h + 2)
            nc.vector.tensor_tensor(
                out=products["s"][:, part, :], in0=products["x"][:, part, :], in1=products["g"][:, part, :], op=ALU.add
            )

        def root_of(j, bank):
            roots[j] = sbuf([P, P, PACK], F32, name="root%d" % j)
            nc.scalar.activation(
                out=roots[j][:], in_=bank[:].rearrange("p (t a) -> p a t", t=PACK), func=ACT.Sqrt, bias=EPS
            )

        nrm = sbuf([P, S, PACK], BF16, name="nrm", align_bytes=64)

        def scale_norm(j, engine):
            engine.tensor_tensor(
                out=nrm[:, j * P : (j + 1) * P, :], in0=roots[j][:],
                in1=gain_sb[:].unsqueeze(1).to_broadcast([P, P, PACK]), op=ALU.mult,
            )

        def quantize_norm(j0, j1):
            cols = slice(j0 * P, j1 * P)
            nc.vector.quantize_mx(
                out=w_codes["nrm"][:, cols].bitcast(FP8X4),
                scales=w_plane["nrm"][:, cols],
                in_=nrm[:, cols, :].rearrange("p a t -> p (a t)"),
            )

        def project_side(c, h, first, bank):
            for r in range(2):
                project(c, 2 * h + r, "w23", slice(first, first + N), bank[:, r * N : (r + 1) * N])

        def project_pair(c, h, bank_a, bank_b):
            project_side(c, h, N, bank_b)
            project_side(c, h, 0, bank_a)

        def project_last_side(c, first, bank):
            atoms = slice(3 * P, 4 * P)
            project(c, 2, "w23", slice(first, first + N), bank[:, :N])
            for m in range(2):
                cols = slice(first + m * P, first + (m + 1) * P)
                nc.tensor.matmul_mx(
                    out=bank[:, N + m * P : N + (m + 1) * P],
                    lhsT=w_codes["w23"][:, cols].bitcast(FP8X4), lhsT_scale=w_plane["w23"][:, cols],
                    rhs=codes[c][:, atoms].bitcast(FP8X4), rhs_scale=planes[c][ROW0[c] :, atoms],
                    start=True, stop=True,
                )

        def project_last(c, bank_a, bank_b):
            project_last_side(c, N, bank_b)
            project_last_side(c, 0, bank_a)

        def add_last(name, first, second):
            products[name] = sbuf([P, N], F32, name="sum_" + name)
            nc.vector.tensor_tensor(out=products[name][:], in0=first, in1=second, op=ALU.add)

        def gate_last(bank):
            gateds[3] = sbuf([P, 2, P], F32, name="gated3")
            nc.vector.scalar_tensor_tensor(
                out=gateds[3][:], in0=bank[:].rearrange("p (m s) -> p m s", m=2)[:, :, P:], scalar=0.5,
                in1=products["dot"][:].rearrange("p (m s) -> p m s", m=2), op0=ALU.mult, op1=ALU.mult,
            )

        def copy_second(c, h, bank_b):
            seconds[c, h] = sbuf([P, 2 * N], F32, name="second_%s%d" % (c, h))
            nc.scalar.copy(out=seconds[c, h][:], in_=bank_b[:])

        def multiply(c, h, bank_a):
            key = c if c == "x" else (c, h)
            if key not in products:
                products[key] = sbuf([P, TILES if c == "x" else 2, N], F32, name="product_%s%d" % (c, h))
            part = products[key][:, 2 * h : 2 * h + 2, :] if c == "x" else products[key][:]
            nc.vector.tensor_tensor(
                out=part.rearrange("p j m -> p (j m)"),
                in0=bank_a[:], in1=seconds[c, h][:], op=ALU.mult,
            )

        def gate_of(h, bank):
            cols = slice(h * HALF, (h + 1) * HALF)
            for m in range(2):
                w4_cols = slice(m * P, (m + 1) * P)
                w5_cols = slice(N + m * P, N + (m + 1) * P)
                nc.tensor.matmul_mx(
                    out=bank[:, m * HALF : (m + 1) * HALF],
                    lhsT=w_codes["w45"][:, w5_cols].bitcast(FP8X4), lhsT_scale=w_plane["w45"][:, w5_cols],
                    rhs=codes["e"][:, cols].bitcast(FP8X4), rhs_scale=planes["e"][ROW0["e"] :, cols],
                    start=True, stop=False,
                )
                nc.tensor.matmul_mx(
                    out=bank[:, m * HALF : (m + 1) * HALF],
                    lhsT=w_codes["w45"][:, w4_cols].bitcast(FP8X4), lhsT_scale=w_plane["w45"][:, w4_cols],
                    rhs=w_codes["nrm"][:, cols].bitcast(FP8X4), rhs_scale=w_plane["nrm"][:, cols],
                    start=False, stop=True,
                )

        def halve_gate(h, bank, pieces=1, count=1):
            half_gates[h] = sbuf([P, 2, HALF], F32, name="half_gate%d" % h)
            width = HALF // pieces
            for r in range(count):
                nc.scalar.activation(
                    out=half_gates[h][:, :, r * width : (r + 1) * width],
                    in_=bank[:].rearrange("p (m s) -> p m s", m=2)[:, :, r * width : (r + 1) * width],
                    func=ACT.Copy, scale=0.5,
                )

        def add_products(cs, tiles, bank, first, last):
            width = P * len(tiles)
            for c in cs:
                for r, j in enumerate(tiles):
                    for m in range(2):
                        nc.tensor.matmul(
                            out=bank[:, m * width + r * P : m * width + (r + 1) * P],
                            lhsT=(products[c][:, j] if c == "x" else products[c, j // 2][:, j % 2])[:, m * P : (m + 1) * P], rhs=ident[:], is_transpose=True,
                            start=(first and c == cs[0] and r == 0 and m == 0),
                            stop=(last and c == cs[-1] and r == len(tiles) - 1 and m == 1),
                        )

        def gate_dot(tiles, bank):
            width = P * len(tiles)
            h, r = divmod(tiles[0], 2)
            gated = sbuf([P, 2, width], F32, name="gated%d" % tiles[0])
            nc.vector.tensor_tensor(
                out=gated[:], in0=bank[:, : 2 * width].rearrange("p (m s) -> p m s", m=2),
                in1=half_gates[h][:, :, r * P : r * P + width], op=ALU.mult,
            )
            gateds[tiles[0]] = gated

        def add_skip(tiles, engine):
            width = P * len(tiles)
            cols = slice(tiles[0] * P, tiles[0] * P + width)
            gated = gateds[tiles[0]]
            result = sbuf([P, 2, width], F32, name="result%d" % tiles[0])
            engine.tensor_tensor(out=result[:], in0=gated[:], in1=skip_sb[:, :, cols], op=ALU.add)
            nc.sync.dma_start(out=out.rearrange("(m p) s -> p m s", p=P)[:, :, cols], in_=result[:])

        def load_gain():
            tile = sbuf([P, PACK], F32, name="gain_sb")
            nc.sync.dma_start(out=tile[:], in_=gain.rearrange("(p t) o -> p (t o)", t=PACK))
            return tile

        def load_skip():
            tile = sbuf([P, 2, S], F32, name="skip_sb")
            nc.sync.dma_start(out=tile[:], in_=skip.rearrange("(m p) s -> p m s", p=P))
            return tile

        def warm_up():
            warm = sbuf([P, 8], F32, name="warm")
            nc.vector.memset(warm[:, 0:1], 1.0)
            nc.scalar.activation(out=warm[:, 4:5], in_=warm[:, 0:1], func=ACT.Sqrt)

        ident = sbuf([P, P], F32, name="ident")


        warm_up()
        clear_scales("x", nc.vector)
        clear_scales("g", nc.vector)
        clear_scales("d", nc.vector)
        clear_scales("e", nc.vector)
        make_identity(nc, ident[:])
        load_words("x")
        load_scales_q("x", nc.sync)
        load_weight("w1a", w1[:, :N])
        load_weight("w1b", w1[:, N:])
        load_weight("w2", w2)
        load_scales_q("g", nc.sync)
        load_words("g")
        load_weight("w3", w3)
        load_scales_q("d", nc.sync)
        load_words("d")
        load_scales("e", nc.sync)
        load_words("e")
        load_weight("w4", w4)
        load_weight("w5", w5)
        gain_sb = load_gain()
        skip_sb = load_skip()

        interleave("w1", 0, "w1a", "S")
        interleave("w1", 1, "w1b", "V")
        quantize_pair("w1", 0, N)
        quantize_pair("w1", N, 2 * N)
        interleave("w23", 0, "w2", "S")
        interleave("w23", 1, "w3", "G")
        quantize_pair("w23")
        for c in "xgde":
            gather_scales(c)
            for h in ((0, 1) if c == "d" else (None,)):
                gather_words(c, h)
        for n, c in enumerate("xg"):
            for j in range(TILES):
                project_w1(c, j, banks[4 * n + j])
                square(c, j, banks[4 * n + j])
        add_squares("gx", 0, banks[0], True, False)
        for j in (1, 2):
            sum_squares(j, nc.gpsimd)
        for h, (a, b) in enumerate(((2, 3), (4, 5))):
            if h == 0:
                project_pair("x", h, banks[a], banks[b])
            else:
                project_last("x", banks[a], banks[b])
            copy_second("x", h, banks[b])
            multiply("x", h, banks[a])

        interleave("w45", 0, "w4", "G")
        interleave("w45", 1, "w5", "V")
        for j, b in enumerate((1, 6, 7, 3)):
            project_w1("d", j, banks[b])
            square("d", j, banks[b])
        add_squares("s", 1, banks[5], True, False)
        add_squares("d", 0, banks[0], False, True)
        root_of(0, banks[0])
        scale_norm(0, nc.vector)
        quantize_pair("w45")
        project_pair("g", 0, banks[1], banks[6])
        copy_second("g", 0, banks[6])
        add_squares("d", 1, banks[5], False, True)
        root_of(1, banks[5])
        scale_norm(1, nc.gpsimd)
        multiply("g", 0, banks[1])
        project_last_side("g", N, banks[7])
        copy_second("g", 1, banks[7])
        add_squares("sd", 2, banks[2], True, True)
        project_last_side("g", 0, banks[3])
        multiply("g", 1, banks[3])
        root_of(2, banks[2])
        scale_norm(2, nc.vector)
        quantize_norm(0, 2)
        project_side("d", 0, N, banks[0])
        copy_second("d", 0, banks[0])
        add_squares("gxd", 3, banks[4], True, True)
        project_side("d", 0, 0, banks[5])
        multiply("d", 0, banks[5])
        root_of(3, banks[4])
        scale_norm(3, nc.vector)
        add_last("xg", products["x"][:, 3], products["g", 1][:, 1])
        quantize_norm(2, 4)
        project_last("d", banks[2], banks[6])
        copy_second("d", 1, banks[6])
        multiply("d", 1, banks[2])
        gate_of(0, banks[7])
        halve_gate(0, banks[7])
        add_products("dxg", [0, 1], banks[1], True, True)
        gate_of(1, banks[0])
        halve_gate(1, banks[0], 2, 1)
        gate_dot([0, 1], banks[1])
        add_last("dot", products["xg"][:], products["d", 1][:, 1])
        add_skip([0, 1], nc.vector)
        add_products("dgx", [2], banks[3], True, True)
        gate_last(banks[0])
        gate_dot([2], banks[3])
        add_skip([3], nc.vector)
        add_skip([2], nc.vector)
